import numpy as np, ml_dtypes
CORES = [25,29,65,69,153,157,193,197]
N = 8
BF = ml_dtypes.bfloat16
S, D, H, CAP = 2560, 2, 128, 2048
def heads(x):
    return x.astype(np.float32).reshape(N, 8, 16, S)
def scores(z, v, t):
    return np.einsum("rgcs,rgc->rgs", z, v[:, :, t].astype(np.float32).reshape(N, 8, 16))
def layer(z, kept, w, gap, t):
    out = z.copy()
    for g in range(8):
        q = np.concatenate([z[r, g][:, kept[r][g]] for r in range(N)], axis=1)
        q = np.pad(q, ((0, 0), (H, H))); a = H
        for r in range(N):
            k = kept[r][g].size; d = int(gap[r, 16 * g, t])
            m = w[r, 16 * g:16 * g + 16, 48 * t:48 * t + 48].astype(np.float32)
            s = m[:, :16].T @ q[:, a:a + k] + m[:, 16:32].T @ q[:, a - d:a - d + k] + m[:, 32:].T @ q[:, a + d:a + d + k]
            out[r, g][:, kept[r][g]] = np.clip(np.rint(s * np.float32(0.125)), -15, 15)
            a += k
    return out
def run(x, v, w, th, gap):
    z = heads(x); kept = [[np.arange(S)] * 8 for r in range(N)]; cnt = np.zeros((D, N, 8), np.int64)
    for t in range(D):
        s = scores(z, v, t)
        kept = [[kept[r][g][s[r, g, kept[r][g]] >= th[r, 16 * g, t]] for g in range(8)] for r in range(N)]
        for r in range(N):
            for g in range(8): cnt[t, r, g] = kept[r][g].size
        z = layer(z, kept, w, gap, t)
    return z, cnt
def rows16(a):
    return np.repeat(a, 16, axis=1).astype(np.int32)
def shares(rng):
    k = [rng.integers(CAP // 2, CAP * 7 // 8 + 1, (N, 8))]
    for t in range(1, D): k.append(np.maximum(k[-1] * rng.integers(60, 91, (N, 8)) // 100, H))
    return np.stack(k)
def settle(d, want):
    x, v, w, gap = d["x"], d["v"], d["w"], d["gap"]
    z = heads(x); kept = [[np.arange(S)] * 8 for r in range(N)]; th = np.zeros((N, 8, D), np.int32)
    for t in range(D):
        s = scores(z, v, t)
        for r in range(N):
            for g in range(8):
                a = s[r, g, kept[r][g]]; e = np.sort(a)[::-1]; lim = int(e[min(int(want[t, r, g]), e.size) - 1])
                if np.count_nonzero(a >= lim) > CAP: lim += 1
                th[r, g, t] = lim; kept[r][g] = kept[r][g][a >= lim]
        z = layer(z, kept, w, gap, t)
    d["th"] = rows16(th); return d
def setup_inputs(rng):
    d = {"x": rng.integers(-15, 16, (N, 128, S)).astype(np.float32).astype(BF), "v": rng.integers(-7, 8, (N, 128, D)).astype(np.float32).astype(BF),
         "w": (2 * rng.integers(0, 2, (N, 128, 48 * D)) - 1).astype(np.float32).astype(BF), "th": None, "gap": rows16(rng.integers(1, H + 1, (N, 8, D)))}
    return settle(d, shares(rng))
def setup_inputs_caps(rng):
    d = setup_inputs(rng); x = d["x"]; s = scores(heads(x), d["v"], 0); g8 = np.arange(8)
    big = (np.arange(N)[:, None] + g8 + rng.integers(0, 2)) % 2 == 0
    for r in range(N):
        for g in range(8):
            k = CAP if big[r, g] else H; u = s[r, g]; o = np.argsort(-u, kind="stable"); late = o[k:]; late = late[u[late] == u[o[k - 1]]]
            b = x[r, 16 * g:16 * g + 16]; b[:, late] = b[:, o[-1:]]
    want = np.stack([np.where(big, CAP, H)] + [np.where(big & (g8 % 4 < 2), CAP, H)] * (D - 1))
    d["gap"] = rows16(rng.choice(np.array([1, H]), (N, 8, D))); return settle(d, want)
def setup_inputs_ends(rng):
    d = setup_inputs(rng); x = d["x"]; s = scores(heads(x), d["v"], 0); k = int(rng.integers(0, 3))
    for r in range(N):
        for g in range(8):
            o = np.argsort(-s[r, g], kind="stable"); m = (r + g + k) % 3
            if m == 1: o = o[::-1]
            if m == 2: o = np.concatenate([o[0::2], o[1::2][::-1]])
            x[r, 16 * g:16 * g + 16] = x[r, 16 * g:16 * g + 16][:, o]
    d["gap"] = rows16(rng.choice(np.array([1, H]), (N, 8, D))); return settle(d, shares(rng))
def setup_inputs_ties(rng):
    d = setup_inputs(rng); c = rng.integers(0, 16, (N, 8, 1, D)); sg = 2 * rng.integers(0, 2, (N, 8, 1, D)) - 1
    d["v"] = ((np.arange(16)[:, None] == c) * sg).reshape(N, 128, D).astype(np.float32).astype(BF)
    return settle(d, shares(rng))
def setup_inputs_spread(rng):
    d = setup_inputs(rng); m = rng.integers(0, 16, (N, 8, 1, S))
    d["x"] = np.rint((2 * rng.random((N, 8, 16, S)) - 1) * m).reshape(N, 128, S).astype(np.float32).astype(BF)
    return settle(d, shares(rng))
def check_inputs(d):
    bad = []; x, v, w = [np.asarray(d[k]).astype(np.float32) for k in ("x", "v", "w")]; th, gap = d["th"], d["gap"]
    if not ((np.rint(x) == x) & (np.abs(x) <= 15)).all(): bad.append("x_whole_within_15")
    if not ((np.rint(v) == v) & (np.abs(v) <= 7)).all(): bad.append("v_whole_within_7")
    if not (np.abs(w) == 1).all(): bad.append("w_one_or_minus_one")
    a = th.reshape(N, 8, 16, D); b = gap.reshape(N, 8, 16, D)
    if (a != a[:, :, :1]).any() or (th < -4096).any() or (th > 4096).any(): bad.append("th")
    if (b != b[:, :, :1]).any() or (gap < 1).any() or (gap > H).any(): bad.append("gap")
    if bad: return bad
    cnt = run(x, v, w, th, gap)[1]
    if cnt.min() < H or cnt.max() > CAP: bad.append("numbers_kept")
    return bad
def reference(x, v, w, th, gap):
    z, cnt = run(x, v, w, th, gap)
    return {"y": z.reshape(N, 128, S).astype(np.float32)}

@@ -1,0 +1,652 @@
+from concourse.mybir import AluOpType, ActivationFunctionType
+
+A = AluOpType
+F = ActivationFunctionType
+
+S, D, H, CAP = 2560, 2, 128, 2048
+NT = S // 16
+COV = H + 16
+NZ = CAP + 16
+NS = NZ // 16
+CH = 448
+MID = 4 * CH
+NE = H + COV
+NW = 2 * COV + CAP + H + 16
+OFF = 192.0
+BIG = 65536.0
+XA = 1536
+YCUT = [0, 768, 1536, 2048, 2560]
+LH1 = 2 * NT + 2
+
+PLAN0 = (["c0", "m3", "x1", "p2", "e3", "p0", "x2", "e0", "e1", "Ee", "e2", "x5"],
+         ["c3", "c2", "c1", "p3", "m1", "p1", "m0", "m2", "Es", "Ev", "x6"],
+         ["M3", "M1", "M0", "EM", "M2", "x3", "x4"])
+PLAN1 = (["y2", "c3", "c2", "x2", "x3", "Es", "x4", "e0", "Ee", "m2", "e1", "f1", "e2", "e3", "f6", "f4"],
+         ["y3", "c0", "c1", "p0", "p2", "m0", "m1", "Ev", "p1", "f0", "m3", "p3", "f2", "f5", "f3"],
+         ["x1", "M0", "EM", "M1", "M2", "M3"])
+FCUT = [0, 576, 1024, 1472, 1728, 1984, 2272, 2560]
+FNEED = [0, 1, 2, 3, 3, 3, 3]
+STORES = [[0], [1], [2], [3, 4, 5, 6]]
+
+SCRATCH = {
+    "xs": ("sbuf", [128, S], "bfloat16"),
+    "xz": ("sbuf", [128, NZ + S], "bfloat16"),
+    "yz": ("sbuf", [128, NZ + S], "bfloat16"),
+    "w0": ("sbuf", [128, NW], "bfloat16"),
+    "w1": ("sbuf", [128, NW], "bfloat16"),
+    "xm": ("sbuf", [128, MID], "bfloat16"),
+    "xp": ("sbuf", [128, MID], "bfloat16"),
+    "xme": ("sbuf", [128, NE], "bfloat16"),
+    "xpe": ("sbuf", [128, NE], "bfloat16"),
+    "ysb": ("sbuf", [128, S], "float32"),
+    "rl0": ("sbuf", [128, COV], "bfloat16"),
+    "rl1": ("sbuf", [128, COV], "bfloat16"),
+    "ro0": ("sbuf", [128, 4], "float32"),
+    "ro1": ("sbuf", [128, 4], "float32"),
+    "ri0": ("sbuf", [128, 4], "float32"),
+    "ri1": ("sbuf", [128, 4], "float32"),
+    "vs": ("sbuf", [128, 2], "bfloat16"),
+    "ths": ("sbuf", [128, 2], "int32"),
+    "gps": ("sbuf", [128, 2], "int32"),
+    "ws": ("sbuf", [128, 6, 16], "bfloat16"),
+    "wm": ("sbuf", [128, 6, 128], "bfloat16"),
+    "sc": ("sbuf", [128, 288], "bfloat16"),
+    "ki": ("sbuf", [128, 4], "int32"),
+    "col": ("sbuf", [128, 32], "float32"),
+    "g8": ("sbuf", [128, 8], "float32"),
+    "b8": ("sbuf", [128, 8], "float32"),
+    "b8s": ("sbuf", [128, 8], "float32"),
+    "gm": ("sbuf", [128, 128], "bfloat16"),
+    "one16": ("sbuf", [128, 128], "bfloat16"),
+    "neg16": ("sbuf", [128, 128], "bfloat16"),
+    "up16": ("sbuf", [128, 128], "bfloat16"),
+    "up16b": ("sbuf", [128, 128], "bfloat16"),
+    "idn": ("sbuf", [128, 128], "bfloat16"),
+    "idb": ("sbuf", [128, 128], "bfloat16"),
+    "tm1": ("sbuf", [128, 128], "bfloat16"),
+    "c15": ("sbuf", [128, 128], "bfloat16"),
+    "ones": ("sbuf", [128, CH], "bfloat16"),
+    "r3": ("sbuf", [128, 8, 32], "bfloat16"),
+    "b3": ("sbuf", [128, 8, 32], "bfloat16"),
+    "bd": ("sbuf", [128, 8, 32], "bfloat16"),
+    "rot": ("sbuf", [128, 16, 8, 16], "bfloat16"),
+    "j16": ("sbuf", [128, NT], "bfloat16"),
+    "nt": ("sbuf", [128, NT], "float32"),
+    "nq0": ("sbuf", [128, NT], "float32"),
+    "nq1": ("sbuf", [128, NT], "float32"),
+    "th16": ("sbuf", [128, 16], "float32"),
+    "ecst": ("sbuf", [128, 10], "float32"),
+    "lmid": ("sbuf", [128, 4 * 28], "uint16"),
+    "mk0": ("sbuf", [128, NT], "bfloat16"),
+    "mk1": ("sbuf", [128, NT], "bfloat16"),
+    "mk2": ("sbuf", [128, NT], "bfloat16"),
+    "vld": ("sbuf", [128, NS], "bfloat16"),
+    "cx": ("sbuf", [128, NT + 1], "bfloat16"),
+    "cy": ("sbuf", [128, NT + 1], "bfloat16"),
+    "ai": ("sbuf", [128, NT], "int32"),
+    "xf": ("sbuf", [128, NT], "bfloat16"),
+    "tt": ("sbuf", [128, 15 * NT], "bfloat16"),
+    "ap": ("sbuf", [128, NT + 1], "bfloat16"),
+    "aq": ("sbuf", [128, NT], "float32"),
+    "aq1": ("sbuf", [128, NT], "float32"),
+    "sgn": ("sbuf", [128, 9 * NT], "bfloat16"),
+    "acc": ("sbuf", [128, 10], "float32"),
+    "el": ("sbuf", [128, 10], "uint16"),
+    "flo": ("sbuf", [128, NT], "float32"),
+    "fhi": ("sbuf", [128, NT], "float32"),
+    "lh": ("sbuf", [128, LH1 + 2 * NS + 2], "float32"),
+    "mx": ("sbuf", [128, NT + 1], "float32"),
+    "lw": ("sbuf", [128, 144], "uint16"),
+    "du": ("sbuf", [128, NT], "float32"),
+    "dl0": ("sbuf", [128, NT], "uint16"),
+    "dl1": ("sbuf", [128, NT], "uint16"),
+    "kt": ("sbuf", [128, 17], "float32"),
+    "et": ("sbuf", [128, 17], "float32"),
+    "eu": ("sbuf", [128, 17], "float32"),
+    "lpl": ("sbuf", [128, 18], "uint16"),
+    "ldy": ("sbuf", [128, 18], "uint16"),
+    "px": ("psum", [128, 512], "float32"),
+    "py": ("psum", [128, 512], "float32"),
+    "pz": ("psum", [128, 512], "float32"),
+    "pe": ("psum", [128, 512], "float32"),
+    "pm0": ("psum", [128, 512], "float32"),
+    "pm1": ("psum", [128, 512], "float32"),
+    "pm2": ("psum", [128, 512], "float32"),
+    "pm3": ("psum", [128, 512], "float32"),
+}
+SEMAPHORES = ["cV", "cS", "cP", "cG", "dxa", "dxb", "dv", "dw", "dst", "sent",
+              "aE0", "aE1", "aC0", "aC1", "aR0", "aR1", "rC0", "rC1", "rR0", "rR1"]
+
+
+def n_eng(m):
+    return bin(m).count("1")
+
+
+def far_rank(r, n):
+    f = r + 1 if r % 2 else r - 1
+    return f if 0 <= f < n else None
+
+
+def relay_of(src, dst, cores, topo):
+    if topo.may_write(src, dst):
+        return None
+    c = [k for k in topo.cores_of(src) if k not in cores and topo.may_write(k, dst)]
+    c.sort(key=lambda k: topo.die(k) != topo.die(src))
+    return c[0]
+
+
+def layout(r):
+    if r % 2:
+        return 0, H + CAP, H, H + CAP + COV
+    return 0, COV, 2 * COV, 2 * COV + CAP
+
+
+def far_landing(T, t, r):
+    lh, _, _, rh = layout(r)
+    a = rh if r % 2 else lh
+    return T["w%d" % t][:, a:a + COV]
+
+
+def relay_program(g, core, T, topo, dst_rank):
+    dst = T.cores[dst_rank]
+    rid, pid = topo.addr(dst, core)
+    m = topo.mask(core, dst)
+    nin = n_eng(topo.mask(T.cores[far_rank(dst_rank, len(T.cores))], core))
+    for t in range(D):
+        g.wait_ge(T.sem["rR%d" % t], nin)
+        g.remote_dma(T["ri%d" % t][:, 0:1], T["ri%d" % t][:, 0:1], T.sem["aR%d" % t], T.sem.sent, pid, rid, m)
+        g.wait_ge(T.sem["rC%d" % t], nin)
+        g.remote_dma(far_landing(T, t, dst_rank), T["rl%d" % t][:], T.sem["aC%d" % t], T.sem.sent, pid, rid, m)
+    g.wait_ge(T.sem.sent, 2 * D * n_eng(m))
+
+
+def rank_program(g, core, T, topo):
+    cores = list(T.cores)
+    n = len(cores)
+    r = T.rank_of(core)
+    if r is None:
+        for k in range(n):
+            f = far_rank(k, n)
+            if f is not None and relay_of(cores[k], cores[f], cores, topo) == core:
+                relay_program(g, core, T, topo, f)
+        return
+
+    odd = r % 2 == 1
+    far = far_rank(r, n)
+    near = r - 1 if odd else r + 1
+    o16 = 0.0 if odd else 128.0
+    LH, CV, MN, RH = layout(r)
+    base = float(MN) + (0.0 if odd else CAP)
+
+    eng = {"V": g.vector, "S": g.scalar, "P": g.tensor, "G": g, "Y": g.sync}
+    cnt = {"V": 0, "S": 0, "P": 0, "G": 0}
+    seen = {e: {} for e in eng}
+    wr, rd, bank = {}, {}, {}
+    sent = [0]
+
+    def wait(e, toks):
+        need = {}
+        for s, v in toks:
+            need[s] = max(need.get(s, 0), v)
+        for s, v in need.items():
+            if seen[e].get(s, 0) < v:
+                eng[e].wait_ge(T.sem[s], v)
+                seen[e][s] = v
+
+    def deps(e, rk, wk, bk):
+        toks = []
+        for k in rk:
+            toks += wr[k]
+        for k in wk:
+            toks += [x for x in wr.get(k, []) + rd.get(k, []) if not (e == "P" and x[0] == "cP")]
+        for k in bk:
+            toks += [(s, v) for s, v in bank.get(k, {}).items() if s != "c" + e]
+        return toks
+
+    def op(e, call, rk=(), wk=(), bk=()):
+        wait(e, deps(e, rk, wk, bk))
+        cnt[e] += 1
+        call().then_inc(T.sem["c" + e], 1)
+        tok = ("c" + e, cnt[e])
+        for k in rk:
+            rd.setdefault(k, []).append(tok)
+        for k in wk:
+            wr[k] = [tok]
+            rd[k] = []
+        for k in bk:
+            bank.setdefault(k, {})[tok[0]] = tok[1]
+
+    def ts(out, in0, s1, s2, op0, op1, rk, wk, bk=()):
+        if op1 is None:
+            op("V", lambda: g.vector.tensor_scalar(out, in0, s1, None, op0), rk, wk, bk)
+        else:
+            op("V", lambda: g.vector.tensor_scalar(out, in0, s1, s2, op0, op1), rk, wk, bk)
+
+    def tt(out, in0, in1, o, rk, wk, bk=()):
+        op("V", lambda: g.vector.tensor_tensor(out, in0, in1, o), rk, wk, bk)
+
+    def cp(out, in_, rk, wk, bk=()):
+        op("V", lambda: g.vector.tensor_copy(out, in_), rk, wk, bk)
+
+    def ms(ap, c, wk):
+        op("V", lambda: g.vector.memset(ap, c), (), wk)
+
+    def scan(out, d0, d1, op0, rk, wk):
+        op("V", lambda: g.vector.tensor_tensor_scan(out, d0, d1, 0.0, op0, A.max), rk, wk)
+
+    def act(out, in_, f, rk, wk, bk=(), **kw):
+        op("S", lambda: g.scalar.activation(out, in_, f, **kw), rk, wk, bk)
+
+    def lin(out, in_, a, b, rk, wk, bk=()):
+        act(out, in_, F.Identity, rk, wk, bk, scale=a, bias=b)
+
+    def sign(out, in_, a, b, rk, wk):
+        act(out, in_, F.Sign, rk, wk, scale=a, bias=b)
+
+    def mm(out, lhsT, rhs, st, sp, rk, wk, bk):
+        op("P", lambda: g.tensor.matmul(out, lhsT, rhs, st, sp), rk, wk, bk)
+
+    def iota(out, pat, cm, wk, fl=True):
+        if fl:
+            op("G", lambda: g.iota(out, pat, 0, cm, allow_small_or_imprecise_dtypes=True), (), wk)
+        else:
+            op("G", lambda: g.iota(out, pat, 0, cm), (), wk)
+
+    def sel(out, in_, cmp, fill, rk, wk):
+        op("G", lambda: g.affine_select(out, in_, [[-1, 128]], cmp, fill, 0, 1), rk, wk)
+
+    def gather(e, out, win, lst, add, rk, wk):
+        src = win.indirect(lst)
+        if e == "V":
+            if add:
+                ts(out, src, add, None, A.add, None, rk, wk)
+            else:
+                cp(out, src, rk, wk)
+        elif add:
+            act(out, src, F.Identity, rk, wk, bias=add)
+        else:
+            act(out, src, F.Copy, rk, wk)
+
+    def clip(out, in_, wk, b):
+        ts(out, in_, OFF + 15, OFF - 15, A.min, A.max, [b], wk, [b])
+
+    def send(dst, out, in_, sem, rk):
+        wait("G", deps("G", rk, (), ()))
+        rid, pid = topo.addr(dst, core)
+        m = topo.mask(core, dst)
+        g.remote_dma(out, in_, T.sem[sem], T.sem.sent, pid, rid, m)
+        sent[0] += n_eng(m)
+
+    names = ["i", "g", "ci", "q0", "q1", "f9", "c0", "th0", "th1", "th1p", "th1b", "d0", "d1", "s0", "s1", "i1",
+             "b0", "kk", "nk", "na", "cc", "dd", "dl", "lim", "h1", "h2"]
+
+    def C(k, w=1):
+        j = names.index(k)
+        return T.col[:, j:j + w]
+
+    g.sync.dma_start(T.xs[:, 0:XA], T.x[:, 0:XA]).then_inc(T.sem.dxa, 16)
+    g.scalar.dma_start(T.vs[:], T.v[:]).then_inc(T.sem.dv, 16)
+    g.sync.dma_start(T.xs[:, XA:S], T.x[:, XA:S]).then_inc(T.sem.dxb, 16)
+    g.scalar.dma_start(T.ths[:], T.th[:]).then_inc(T.sem.dw, 16)
+    g.scalar.dma_start(T.ws[:], T.w[:]).then_inc(T.sem.dw, 16)
+    g.scalar.dma_start(T.gps[:], T.gap[:]).then_inc(T.sem.dw, 16)
+    wr["xa"], wr["xb"], wr["vs"] = [("dxa", 16)], [("dxb", 16)], [("dv", 16)]
+    wr["ths"] = wr["ws"] = wr["gps"] = [("dw", 48)]
+    for t in range(D):
+        wr["near%d" % t] = [("aE%d" % t, n_eng(topo.mask(cores[near], core)))]
+        if far is not None:
+            rl = relay_of(cores[far], core, cores, topo)
+            k = n_eng(topo.mask(cores[far] if rl is None else rl, core))
+            wr["far%d" % t], wr["ri%d" % t] = [("aC%d" % t, k)], [("aR%d" % t, k)]
+
+    dconst = [8191.0 if odd else 8191.0 + CAP + 16, float(S + COV - 8193) if odd else 8191.0 + CAP - H]
+
+    iota(T.ki[:, 0:1], [[0, 1]], 1, ["ki0"], False)
+    iota(T.g8[:], [[1, 8]], 0, ["g8"])
+    iota(T.gm[:], [[1, 8], [0, 16]], 0, ["gm"])
+    iota(T.r3[:], [[-16, 8], [0, 2], [-1, 16]], 1, ["r3"])
+    iota(T.j16[:], [[16, NT]], 0, ["j16"])
+    ms(T.sc[:], 0.0, ["sc0", "sc1"])
+    ts(T.ki[:, 1:2], T.ki[:, 0:1], 4, None, A.arith_shift_right, None, ["ki0"], ["ki1"])
+    ts(T.ki[:, 2:3], T.ki[:, 0:1], 15, None, A.bitwise_and, None, ["ki0"], ["ki2"])
+    ms(T.ones[:], 1.0, ["ones"])
+    cp(C("g"), T.ki[:, 1:2], ["ki1"], ["g"])
+    cp(C("i"), T.ki[:, 2:3], ["ki2"], ["i"])
+    ms(T.c15[:], OFF / 128, ["c15"])
+    ts(T.neg16[:], T.gm[:], C("g"), -0.0625, A.is_equal, A.mult, ["gm", "g"], ["neg16"])
+    ts(T.b8[:], T.g8[:], C("g"), None, A.is_equal, None, ["g8", "g"], ["b8"])
+    ts(T.b3[:], T.r3[:], 0.0, C("i"), A.is_equal, A.mult, ["r3", "i"], ["b3"])
+    ts(T.one16[:], T.gm[:], C("g"), 0.0625, A.is_equal, A.mult, ["gm", "g"], ["one16"])
+    ts(T.sc[:, 15:143:16], T.b8[:], T.vs[:, 0:1], None, A.mult, None, ["b8", "vs"], ["sc0"])
+    tt(T.bd[:, :, 1:32], T.b3[:, :, 1:32], T.b3[:, :, 0:31], A.subtract, ["b3"], ["bd"])
+    ts(T.nt[:], T.j16[:], C("i"), None, A.add, None, ["j16", "i"], ["nt"])
+    sel(T.tm1[:], T.neg16[:], A.is_gt, 0.0, ["neg16"], ["tm1"])
+    sel(T.idn[:], T.ones[:, 0:128], A.is_equal, 0.0, ["ones"], ["idn"])
+    sel(T.up16[:], T.tm1[:], A.not_equal, -512.0, ["tm1"], ["up16"])
+    for k in range(8, 15):
+        op("G", lambda: g.affine_select(T.rot[:, k], T.bd[:, :, 16 - k:32 - k], [[0, 8], [0, 16]], A.is_gt, 0.0, 1, 0),
+           ["bd"], ["rot%d" % k])
+    if odd:
+        sel(T.up16b[:], T.tm1[:], A.not_equal, 512.0, ["tm1"], ["up16b"])
+    lin(T.b8s[:], T.b8[:], 0.125, 0.0, ["b8"], ["b8s"])
+    lin(C("ci"), C("i"), -0.0625, -0.0625 - 0.47, ["i"], ["ci"])
+    lin(C("i1"), C("i"), 0.0625, 0.0625, ["i"], ["i1"])
+    lin(C("q0"), C("i"), 0.0625, -129.0 - o16, ["i"], ["q0"])
+    lin(C("q1"), C("i"), 0.0625, -128.0 - o16, ["i"], ["q1"])
+    act(T.rot[:, 15], T.b3[:, :, 1:17], F.Copy, ["b3"], ["rot15"])
+    lin(T.th16[:], T.j16[:, 0:16], 1.0 / 256, C("i1"), ["j16", "i1"], ["th16"])
+    ms(T.cx[:, 0:1], 0.0, ["cx0"])
+    ms(T.lh[:, NT:LH1 + NS + 1:LH1 + NS - NT], 0.0, ["lhz"])
+    for t in range(D):
+        ms(T["w%d" % t][:, NW - 16:NW], 0.0, ["pad%d" % t])
+        if far is None:
+            ms(far_landing(T, t, r), 0.0, ["far%d" % t])
+            ms(T["ri%d" % t][:], 0.0, ["ri%d" % t])
+    ts(C("f9"), C("i"), 9.0, None, A.is_lt, None, ["i"], ["f9"])
+    cp(C("th0", 2), T.ths[:], ["ths"], ["th0", "th1"])
+    cp(C("d0", 2), T.gps[:], ["gps"], ["d0", "d1"])
+    ts(T.sc[:, 159:287:16], T.b8[:], T.vs[:, 1:2], None, A.mult, None, ["b8", "vs"], ["sc1"])
+    for k in range(8):
+        act(T.wm[:, :, 16 * k:16 * k + 16], T.ws[:], F.Copy, ["ws", "b8s"], ["wm%d" % k], scale=T.b8s[:, k:k + 1])
+    WM = ["wm%d" % k for k in range(8)]
+    lin(T.ecst[:], T.nt[:, 0:10], 1.0, -9.0 - o16 - 1.0 / 32, ["nt"], ["ecst"])
+    for k in range(8):
+        act(T.rot[:, k], T.bd[:, :, 16 - k:32 - k], F.Copy, ["bd"], ["rot%d" % k])
+    lin(C("c0"), C("f9"), -119.0 - (8.0 if odd else 0.0), T.ecst[:, 0:1], ["f9", "ecst"], ["c0"])
+    lin(C("s0", 2), C("d0", 2), 1.0 if odd else -1.0, 0.0, ["d0", "d1"], ["sd"])
+    if odd:
+        lin(T.kt[:, 9:17], T.nt[:, 0:8], 1.0, 0.0, ["nt"], ["kts"])
+    else:
+        lin(T.kt[:, 0:8], T.nt[:, 0:8], 1.0, -128.0, ["nt"], ["kts"])
+    mm(T.pm3[:, 500:502], T.one16[:], T.vs[:], True, True, ["one16", "vs"], ["sumv"], ["pm3"])
+    lin(C("th1p"), T.pm3[:, 501:502], 16 * OFF, C("th1"), ["sumv", "th1"], ["th1p"], ["pm3"])
+    lin(T.nq0[:], T.nt[:], 0.0625, (NZ - dconst[0]) / 16, ["nt"], ["nq0"])
+    lin(T.idb[:], T.idn[:], BIG, 0.0, ["idn"], ["idb"])
+    lin(C("th1b"), C("th1p"), 1.0, BIG, ["th1p"], ["th1b"])
+
+    def offsets_mm(banks):
+        for b, w in banks:
+            mm(T[b][:, 0:w], T.c15[:], T.ones[:, 0:w], True, False, ["c15", "ones"], [b], [b])
+
+    def scores(t, out, src, a, b, rk, flags=None):
+        if flags is not None:
+            mm(out, T.idb[:], flags[0], True, False, ["idb"] + flags[1], ["sco"], ["px"])
+        for i in range(16):
+            u = 144 * t + 15 - i
+            mm(out, T.sc[:, u:u + 128], src[:, a + i:b:16], i == 0 and flags is None, i == 15,
+               ["sc%d" % t] + rk, ["sco"], ["px"])
+
+    def prefix(nc, m, up):
+        mk = T[m][:, 0:nc]
+        mm(T.px[:, NT:NT + nc], T[up][:], mk, True, False, [up, m], ["val"], ["px"])
+        scan(T.cx[:, 1:nc + 1], mk, mk, A.add, [m], ["cx"])
+        c, ck = T.cx, ["cx", "cx0"]
+        if not odd:
+            ts(T.cy[:, 0:nc + 1], T.cx[:, 0:nc + 1], T.cx[:, nc:nc + 1], None, A.subtract, None, ck, ["cy"])
+            c, ck = T.cy, ["cy"]
+        mm(T.px[:, NT:NT + nc], T.one16[:], c[:, 1:nc + 1], False, True, ["one16"] + ck, ["val"], ["px"])
+        return c, ck
+
+    def ktc(a, b):
+        o = 0 if odd else 8
+        return T.kt[:, o + a:o + b]
+
+    def lists(t, nc, s_after):
+        m = "mk%d" % t
+        mm(T.pz[:, 0:nc], T.idn[:], T.j16[:, 0:nc], True, False, ["idn", "j16"], ["rr"], ["pz"])
+        c, ck = prefix(nc, m, "up16")
+        mm(T.py[:, 0:nc + 1], T.one16[:], c[:, 0:nc + 1], True, True, ["one16"] + ck, ["py"], ["py"])
+        mm(T.pe[:, 0:nc + 1], T.one16[:], c[:, 0:nc + 1], True, True, ["one16"] + ck, ["pe"], ["pe"])
+        mm(T.pz[:, 0:nc], T.rot[:, 15], T[m][:, 0:nc], False, False, ["rot15", m], ["rr"], ["pz"])
+        for k, o in ((0, A.subtract), (1, A.add)):
+            a = 56 * t + 28 * k
+            ts(T.lmid[:, a:a + 28], T.nt[:, 0:28], C("d%d" % t), 128.0, o, A.add, ["nt", "d%d" % t],
+               ["lmid%d%d" % (t, k)])
+        val = T.px[:, NT:NT + nc]
+        kc = nc if odd else 0
+        ro, apk, pk = T["ro%d" % t][:, 0:1], T.ap[:, kc:kc + 1], T.py[:, kc:kc + 1]
+        ab = 129.0 + o16
+        act(T.ap[:, 0:nc + 1], T.py[:, 0:nc + 1], F.Identity, ["py"], ["ap"], ["py"], bias=ab - 0.47)
+
+        def count(k):
+            act(T.sgn[:, k * NT:k * NT + nc], T.py[:, 1:nc + 1], F.Sign, ["py", "ecst" if k else "b0"],
+                ["acc%d" % k], ["py"], bias=T.ecst[:, k:k + 1] if k else C("b0"), scale=-1.0,
+                accum_out=T.acc[:, k:k + 1])
+
+        count(1)
+        lin(C("na"), apk, -16.0, 16 * ab, ["ap"], ["na"])
+        lin(C("b0"), apk, C("f9"), C("c0"), ["ap", "f9", "c0"], ["b0"])
+        lin(ro, pk, 16.0, C("na"), ["py", "na"], ["ro%d" % t], ["py"])
+        if far is not None:
+            rl = relay_of(core, cores[far], cores, topo)
+            send(cores[far] if rl is None else rl, T["ri%d" % t][:, 0:1], ro,
+                 ("aR%d" if rl is None else "rR%d") % t, ["ro%d" % t])
+        lin(T.aq[:, 0:nc], T.ap[:, 0:nc], 1.0, C("q0"), ["ap", "q0"], ["aq"])
+        lin(T.aq1[:, 0:nc], T.ap[:, 0:nc], 1.0, C("q1"), ["ap", "q1"], ["aq1"])
+        for k in (2, 3, 4, 5, 6, 7, 8, 0):
+            count(k)
+        cc = (-8.0 + (8193.0 / 16 if t else -8191.0 / 16)) if odd else 9.0 - 8191.0 / 16
+        dd = (-1.0 if t else 128.0) if odd else (0.0 if t else -129.0)
+        lin(C("lim"), apk, 16.0, -16 * ab - (128.0 if odd else 0.0), ["ap"], ["lim"])
+        lin(C("cc"), apk, 1.0, cc - ab, ["ap"], ["cc"])
+        lin(C("dd"), apk, -1.0, dd + ab, ["ap"], ["dd"])
+        lin(ktc(0, 9), T.nt[:, 0:9], 1.0, C("lim"), ["nt", "lim"], ["ktc"])
+        lin(C("kk"), pk, 16.0, 0.0, ["py"], ["kk"], ["py"])
+        lin(C("nk"), pk, -16.0, (RH if odd else H) - base, ["py"], ["nk"], ["py"])
+        lin(T.et[:], T.kt[:], 1.0, C("s%d" % t), ["kts", "ktc", "sd"], ["et"])
+        s_after()
+
+        def slot_flags():
+            if odd:
+                lin(C("h1"), apk, 16.0, -16 * ab - 128.5, ["ap"], ["h1"])
+                lin(C("h2"), pk, 16.0, -0.5, ["py"], ["h2"], ["py"])
+                sign(T.vld[:, 0:120], T.nt[:, 0:120], -1.0, C("h1"), ["nt", "h1"], ["vla"])
+                sign(T.vld[:, 120:NS], ktc(0, 9), -1.0, C("h2"), ["ktc", "h2"], ["vlb", "vlc"])
+            else:
+                lin(C("h1"), apk, -16.0, 16 * ab - CAP - COV + 0.5, ["ap"], ["h1"])
+                lin(C("h2"), pk, -16.0, 0.5, ["py"], ["h2"], ["py"])
+                sign(T.vld[:, 8:9], ktc(8, 9), -1.0, -0.5, ["ktc"], ["vlc"])
+                sign(T.vld[:, 9:NS], T.nt[:, 8:128], 1.0, C("h1"), ["nt", "h1"], ["vla"])
+                sign(T.vld[:, 0:8], ktc(0, 8), 1.0, C("h2"), ["ktc", "h2"], ["vlb"])
+            lin(T.nq1[:], T.nt[:], 0.0625, ((0 if odd else NZ) - dconst[1]) / 16, ["nt"], ["nq1"])
+
+        ts(T.ai[:, 0:nc], val, C("ci"), -300.0, A.add, A.min, ["val", "ci"], ["ai"], ["px"])
+        tt(T.xf[:, 0:nc], val, T.ai[:, 0:nc], A.subtract, ["val", "ai"], ["xf"], ["px"])
+        for k in range(15):
+            tk = T.tt[:, k * NT:k * NT + nc]
+            ts(tk, T.xf[:, 0:nc], T.th16[:, k:k + 1], None, A.is_le, None, ["xf", "th16"], ["t%d" % k])
+            mm(T.pz[:, 0:nc], T.rot[:, k], tk, False, k == 14, ["rot%d" % k, "t%d" % k], ["rr"], ["pz"])
+        tt(T.flo[:, 0:nc], T.pe[:, 0:nc], T.aq[:, 0:nc], A.is_le, ["pe", "aq"], ["flo"], ["pe"])
+        tt(T.fhi[:, 0:nc], T.pe[:, 1:nc + 1], T.aq1[:, 0:nc], A.is_gt, ["pe", "aq1"], ["fhi"], ["pe"])
+        b = LH1 * t
+        tt(T.lh[:, b:b + nc], T.pz[:, 0:nc], T.flo[:, 0:nc], A.mult, ["rr", "flo"], ["lo"], ["pz"])
+        tt(T.lh[:, b + nc + 1:b + 2 * nc + 1], T.pz[:, 0:nc], T.fhi[:, 0:nc], A.mult, ["rr", "fhi"], ["hi"], ["pz"])
+        ts(T.el[:, 0:9], T.acc[:, 0:9], float(nc), 0.5, A.add, A.mult, ["acc%d" % k for k in range(9)], ["el"])
+        scan(T.mx[:, 0:nc + 1], T.lh[:, b:b + nc + 1], T.lh[:, b + nc:b + 2 * nc + 1], A.max,
+             ["lo", "hi", "lhz"], ["mx"])
+        gather("V", T.lw[:], T.mx[:, 0:nc + 1], T.el[:, 0:9], 0, ["mx", "el"], ["lw"])
+        return slot_flags
+
+    def fspan(j):
+        a, b = FCUT[j], FCUT[j + 1]
+        return (a, b) if odd else (S - b, S - a)
+
+    def place_list(t):
+        val, dw = T.px[:, NT:2 * NT], T.pz[:, 0:NT]
+        ts(T.du[:], val, C("cc"), C("dd"), A.is_ge if odd else A.is_lt, A.mult, ["val", "cc", "dd"], ["du"], ["px"])
+        tt(dw, val, T.du[:], A.add, ["val", "du"], ["rr"], ["px", "pz"])
+        tt(T.du[:], dw, T["nq%d" % t][:], A.max if odd and t else A.min, ["rr", "nq%d" % t], ["du"], ["pz"])
+        if odd or t == 0:
+            ts(T["dl%d" % t][:], T.du[:], 16.0, dconst[t], A.mult, A.add, ["du"], ["dl%d" % t])
+        else:
+            for c in range(4):
+                js = [j for j in range(len(FNEED)) if FNEED[j] == c]
+                a, b = fspan(js[-1])[0] // 16, fspan(js[0])[1] // 16
+                ts(T.dl1[:, a:b], T.du[:, a:b], 16.0, dconst[t] - CH * (3 - c), A.mult, A.add, ["du"], ["dl1%d" % c])
+            wr["dl1"] = wr["dl13"]
+
+    def plain_list(t):
+        ts(T.lpl[:, 0:17], T.kt[:], C("s%d" % t), base - (0 if odd else COV), A.subtract, A.add,
+           ["kts", "ktc", "sd"], ["lpl"])
+
+    def far_list(t):
+        ts(C("dl"), T["ri%d" % t][:, 0:1], C("nk"), None, A.add, None, ["ri%d" % t, "nk"], ["dl"])
+        ts(T.eu[:], T.et[:], C("kk"), C("dl"), A.is_ge if odd else A.is_lt, A.mult, ["et", "kk", "dl"], ["eu"])
+        tt(T.eu[:], T.eu[:], T.et[:], A.add, ["et", "eu"], ["eu"])
+        ts(T.ldy[:, 0:17], T.eu[:], base, None, A.add, None, ["eu"], ["ldy"])
+
+    PIECE = [(8, 44), (44, 72), (72, 100), (100, 128)] if odd else [(84, 120), (56, 84), (28, 56), (0, 28)]
+
+    def depth(t, src, sk, add, z, zmid, edge_out, plan, extra):
+        w = T["w%d" % t]
+        wa, wb, wc = T.wm[:, 3 * t, :], T.wm[:, 3 * t + 1, :], T.wm[:, 3 * t + 2, :]
+        K = lambda s: "%s%d" % (s, t)
+        ea = 0 if odd else 120
+        cov = w[:, CV:CV + COV]
+        offsets_mm([("pm%d" % c, CH) for c in (range(4) if t else [3])])
+        gather("V", cov, src, T.lw[:, 0:9], add, sk + ["lw"], [K("cov")])
+        offsets_mm([("pe", NE)])
+        if far is not None:
+            rl = relay_of(core, cores[far], cores, topo)
+            if rl is None:
+                send(cores[far], far_landing(T, t, far), cov, K("aC"), [K("cov")])
+            else:
+                send(rl, T["rl%d" % t][:], cov, K("rC"), [K("cov")])
+        edge = w[:, MN + 16 * ea:MN + 16 * ea + H]
+        gather("V", edge, src, T.lw[:, 10 + ea:18 + ea], add, sk + ["lw"], [K("edg")])
+        nl = layout(near)
+        na = nl[3] if odd else nl[0]
+        send(cores[near], w[:, na:na + H], edge, K("aE"), [K("edg")])
+        plain_list(t)
+        own = [K("c%d_" % j) for j in range(4)] + [K("edg"), K("cov"), K("near")]
+        epl, edy = ("xme", "xpe") if odd else ("xpe", "xme")
+
+        def task(e, name):
+            kind = name[0]
+            if kind in "cmpMe":
+                i = int(name[1])
+                c = i if odd else 3 - i
+                need = [K("c%d_" % i), K("c%d_" % (i - 1)) if i else K("edg")]
+                b = "pm%d" % i
+            if kind == "c":
+                a, b = PIECE[i]
+                gather(e, w[:, MN + 16 * a:MN + 16 * b], src, T.lw[:, 10 + a:10 + b], add, sk + ["lw"],
+                       [K("c%d_" % i)])
+            elif kind in "mp":
+                a = MN + CH * c
+                k = 0 if kind == "m" else 1
+                gather(e, T["x" + kind][:, CH * i:CH * (i + 1)], w[:, a:a + CH + 2 * H],
+                       T.lmid[:, 56 * t + 28 * k:56 * t + 28 * k + 28], 0, need + ["lmid%d%d" % (t, k)], ["x" + name])
+            elif kind == "M":
+                a = MN + H + CH * c
+                mm(T[b][:, 0:CH], wa, w[:, a:a + CH], False, False, WM + need, [b], [b])
+                mm(T[b][:, 0:CH], wb, T.xm[:, CH * i:CH * (i + 1)], False, False, ["xm%d" % i], [b], [b])
+                mm(T[b][:, 0:CH], wc, T.xp[:, CH * i:CH * (i + 1)], False, True, ["xp%d" % i], [b], [b])
+            elif kind == "e":
+                clip(z[:, zmid + CH * c:zmid + CH * (c + 1)], T[b][:, 0:CH], [K("zm%d_" % i)], b)
+            elif name == "Es":
+                if odd:
+                    gather(e, T[epl][:], w[:, 0:RH], T.lpl[:, 0:17], 0, own + ["lpl"], [epl])
+                else:
+                    gather(e, T[epl][:], w[:, COV:NW], T.lpl[:, 0:17], 0, own + [K("pad"), "lpl"], [epl])
+            elif name == "Ev":
+                gather(e, T[edy][:], w[:], T.ldy[:, 0:17], 0, own + [K("pad"), K("far"), "ldy"], [edy])
+            elif name == "EM":
+                p1, p2, e1 = (cov, edge, COV) if odd else (edge, cov, H)
+                mm(T.pe[:, 0:e1], wa, p1, False, False, WM + [K("edg"), K("cov")], ["pe"], ["pe"])
+                mm(T.pe[:, e1:NE], wa, p2, False, False, WM + [K("edg"), K("cov")], ["pe"], ["pe"])
+                mm(T.pe[:, 0:NE], wb if odd else wc, T[epl][:], False, False, [epl], ["pe"], ["pe"])
+                mm(T.pe[:, 0:NE], wc if odd else wb, T[edy][:], False, True, [edy], ["pe"], ["pe"])
+            elif name == "Ee":
+                for j, (a, b, o) in enumerate(edge_out):
+                    clip(z[:, o:o + b - a], T.pe[:, a:b], [K("ze%d_" % j)], "pe")
+            elif name == "x2":
+                far_list(t)
+            else:
+                extra[name](e)
+
+        pre = {"Es": ["c0", "c1", "c2", "c3"], "Ev": ["c0", "c1", "c2", "c3", "x2"], "EM": ["Es", "Ev"],
+               "Ee": ["EM"]}
+        for i in range(4):
+            pre["m%d" % i] = pre["p%d" % i] = ["c%d" % j for j in range(max(0, i - 1), i + 1)]
+            pre["M%d" % i] = ["m%d" % i, "p%d" % i] + extra["preM"]
+            pre["e%d" % i] = ["M%d" % i]
+        pre.update(extra["pre"])
+        pend = {"V": list(plan[0]), "S": list(plan[1]), "P": list(plan[2])}
+        done = set()
+        while pend["V"] or pend["S"] or pend["P"]:
+            moved = False
+            for e in "VSP":
+                while pend[e] and all(x in done for x in pre.get(pend[e][0], [])):
+                    task(e, pend[e][0])
+                    done.add(pend[e].pop(0))
+                    moved = True
+            assert moved
+
+    offsets_mm([("pm%d" % c, CH) for c in range(3)])
+    scores(0, T.px[:, 0:XA // 16], T.xs, 0, XA, ["xa"])
+    ts(T.xz[:, NZ:NZ + XA], T.xs[:, 0:XA], OFF, None, A.add, None, ["xa"], ["x192a"])
+    scores(0, T.px[:, XA // 16:NT], T.xs, XA, S, ["xb"])
+    ts(T.xz[:, NZ + XA:NZ + S], T.xs[:, XA:S], OFF, None, A.add, None, ["xb"], ["x192b"])
+    ts(T.mk0[:], T.px[:, 0:NT], C("th0"), None, A.is_ge, None, ["sco", "th0"], ["mk0"], ["px"])
+    flags = lists(0, NT, lambda: None)
+    zm = ["zm%d_0" % i for i in range(4)]
+    sa, sb = ((0, 64), (64, NS)) if odd else ((65, NS), (0, 65))
+    eo0 = [(COV, NE, 0), (0, COV, NZ - COV)] if odd else [(0, H, NZ - H), (H, NE, 0)]
+
+    def slot_scores(ab, rk):
+        a, b = ab
+        scores(1, T.px[:, a:b], T.xz, 16 * a, 16 * b, rk, (T.vld[:, a:b], ["vla", "vlb", "vlc"]))
+
+    ex0 = {
+        "x1": lambda e: place_list(0),
+        "x3": lambda e: slot_scores(sa, zm[0:2] + ["ze0_0"]),
+        "x4": lambda e: slot_scores(sb, zm[2:4] + ["ze1_0"]),
+        "x5": lambda e: ts(T.mk1[:, 0:NS], T.px[:, 0:NS], C("th1b"), None, A.is_ge, None, ["sco", "th1b"], ["mk1"],
+                           ["px"]),
+        "x6": lambda e: flags(),
+        "pre": {"x3": ["e0", "e1", "Ee", "x1", "x6"], "x4": ["e2", "e3", "x3"], "x5": ["x4"]},
+        "preM": [],
+    }
+    depth(0, T.xs[:], ["xa", "xb"], 0, T.xz, H if odd else COV, eo0, PLAN0, ex0)
+    z0 = zm + ["ze0_0", "ze1_0"]
+    YB = 0 if odd else NZ
+
+    def expand(j, e):
+        a, b = YCUT[j], YCUT[j + 1]
+        gather(e, T.yz[:, YB + a:YB + b], T.xz[:], T.dl0[:, a // 16:b // 16], 0,
+               z0 + ["x192a", "x192b", "dl0"], ["y1_%d" % j])
+
+    expand(0, "S")
+
+    lists(1, NS, lambda: expand(1, "S"))
+    y1 = ["y1_%d" % j for j in range(4)]
+
+    def final(j):
+        def run(e):
+            a, b = fspan(j)
+            c = FNEED[j]
+            win = T.yz[:, 0:S + NE + CH * (c + 1)] if odd else T.yz[:, CH * (3 - c):NZ + S]
+            gather(e, T.ysb[:, a:b], win, T.dl1[:, a // 16:b // 16], -OFF,
+                   ["zm%d_1" % i for i in range(c + 1)] + ["ze0_1", "dl1"] + y1, ["ysb%d" % j])
+        return run
+
+    ex1 = {
+        "y2": lambda e: expand(2, e),
+        "y3": lambda e: expand(3, e),
+        "x1": lambda e: scores(1, T.px[:, 0:NT], T.yz, YB, YB + S, y1, (T.mk0[:], ["mk0"])),
+        "x3": lambda e: (ts(T.mk2[:], T.px[:, 0:NT], C("th1b"), None, A.is_ge, None, ["sco", "th1b"], ["mk2"], ["px"]),
+                         prefix(NT, "mk2", "up16b" if odd else "up16")),
+        "x4": lambda e: place_list(1),
+        "pre": {"x1": ["y2", "y3"], "x3": ["x1"], "x4": ["x3"]},
+        "preM": ["x3"],
+    }
+    for j in range(len(FNEED)):
+        ex1["f%d" % j] = final(j)
+        ex1["pre"]["f%d" % j] = ["e%d" % i for i in range(FNEED[j] + 1)] + ["Ee", "x4"]
+    depth(1, T.xz[:, 0:NZ], z0, -OFF, T.yz, S + NE if odd else 0, [(0, NE, S if odd else MID)], PLAN1, ex1)
+    for js in STORES:
+        a, b = min(fspan(j)[0] for j in js), max(fspan(j)[1] for j in js)
+        wait("Y", deps("Y", ["ysb%d" % j for j in js], (), ()))
+        g.sync.dma_start(T.y[:, a:b], T.ysb[:, a:b]).then_inc(T.sem.dst, 16)
+    wait("G", [("c" + e, cnt[e]) for e in cnt] + [("sent", sent[0]), ("dst", 16 * len(STORES))])

@@ -8,25 +8,31 @@ NT = S // 16
 COV = H + 16
 NZ = CAP + 16
 NS = NZ // 16
-CH = 448
-MID = 4 * CH
-NE = H + COV
+MID = CAP - H
+CUM = ([0, 512, 1024, 1536, MID], [0, 512, 1024, 1536, 1792, MID])
+BANKS = ["pm0", "pm1", "pm2", "pm3", "pz"]
+CH = 512
 NW = 2 * COV + CAP + H + 16
 OFF = 192.0
 BIG = 65536.0
+U = 8192.0
 XA = 1536
-YCUT = [0, 768, 1536, 2048, 2560]
-LH1 = 2 * NT + 2
+FHI = 7
+XS = 1280
+ENG = (8, 8, 16)
+SC = 256
 
-PLAN0 = (["c0", "m3", "x1", "p2", "e3", "p0", "x2", "e0", "e1", "Ee", "e2", "x5"],
-         ["c3", "c2", "c1", "p3", "m1", "p1", "m0", "m2", "Es", "Ev", "x6"],
-         ["M3", "M1", "M0", "EM", "M2", "x3", "x4"])
-PLAN1 = (["y2", "c3", "c2", "x2", "x3", "Es", "x4", "e0", "Ee", "m2", "e1", "f1", "e2", "e3", "f6", "f4"],
-         ["y3", "c0", "c1", "p0", "p2", "m0", "m1", "Ev", "p1", "f0", "m3", "p3", "f2", "f5", "f3"],
-         ["x1", "M0", "EM", "M1", "M2", "M3"])
-FCUT = [0, 576, 1024, 1472, 1728, 1984, 2272, 2560]
-FNEED = [0, 1, 2, 3, 3, 3, 3]
-STORES = [[0], [1], [2], [3, 4, 5, 6]]
+PLAN0 = ("c1 c2 p1 m2 x1 e1 e2 x2 e0 e3 Ee y0 x5".split(),
+         "c0 c3 m1 p2 p3 p0 m0 m3 Es Ev y1".split(),
+         "A1 A2 M1 A3 M2 A0 x8 M0 M3 EM x3 x4".split())
+PLAN1 = ("y4 c0 p1 m1 x3 m3 x2 e0 e1 Ee f0 f2 p4 e2 m4 e3 e4 f5 f7".split(),
+         "y5 c1 c3 c2 p0 c4 m0 p3 p2 Es Ev m2 f1 f3 f4 f6".split(),
+         "x1 A1 x8 x7 M1 A0 M0 A2 EM A3 M2 M3 A4 M4".split())
+TA = 2560
+YCUT = [0, 352, 1056, 1184, 1600, 2080, 2560]
+FCUT = [0, 128, 256, 512, 1024, 1536, 1792, 2176, 2560]
+FNEED = [0, 0, 0, 1, 2, 3, 4, 4]
+STORES = [[0, 1], [2], [3], [4], [5], [6, 7]]
 
 SCRATCH = {
     "xs": ("sbuf", [128, S], "bfloat16"),
@@ -36,18 +42,17 @@ SCRATCH = {
     "w1": ("sbuf", [128, NW], "bfloat16"),
     "xm": ("sbuf", [128, MID], "bfloat16"),
     "xp": ("sbuf", [128, MID], "bfloat16"),
-    "xme": ("sbuf", [128, NE], "bfloat16"),
-    "xpe": ("sbuf", [128, NE], "bfloat16"),
+    "xme": ("sbuf", [128, COV], "bfloat16"),
+    "xpe": ("sbuf", [128, COV], "bfloat16"),
     "ysb": ("sbuf", [128, S], "float32"),
     "rl0": ("sbuf", [128, COV], "bfloat16"),
     "rl1": ("sbuf", [128, COV], "bfloat16"),
-    "ro0": ("sbuf", [128, 4], "float32"),
-    "ro1": ("sbuf", [128, 4], "float32"),
-    "ri0": ("sbuf", [128, 4], "float32"),
-    "ri1": ("sbuf", [128, 4], "float32"),
+    "ri0": ("sbuf", [128, 8], "bfloat16"),
+    "ri1": ("sbuf", [128, 8], "bfloat16"),
     "vs": ("sbuf", [128, 2], "bfloat16"),
     "ths": ("sbuf", [128, 2], "int32"),
     "gps": ("sbuf", [128, 2], "int32"),
+    "apn": ("sbuf", [128, 2], "bfloat16"),
     "ws": ("sbuf", [128, 6, 16], "bfloat16"),
     "wm": ("sbuf", [128, 6, 128], "bfloat16"),
     "sc": ("sbuf", [128, 288], "bfloat16"),
@@ -55,56 +60,57 @@ SCRATCH = {
     "col": ("sbuf", [128, 32], "float32"),
     "g8": ("sbuf", [128, 8], "float32"),
     "b8": ("sbuf", [128, 8], "float32"),
-    "b8s": ("sbuf", [128, 8], "float32"),
+    "kc": ("sbuf", [128, 4], "bfloat16"),
     "gm": ("sbuf", [128, 128], "bfloat16"),
     "one16": ("sbuf", [128, 128], "bfloat16"),
     "neg16": ("sbuf", [128, 128], "bfloat16"),
     "up16": ("sbuf", [128, 128], "bfloat16"),
     "up16b": ("sbuf", [128, 128], "bfloat16"),
     "idn": ("sbuf", [128, 128], "bfloat16"),
+    "idm": ("sbuf", [128, 128], "bfloat16"),
+    "idh": ("sbuf", [128, 128], "bfloat16"),
     "idb": ("sbuf", [128, 128], "bfloat16"),
     "tm1": ("sbuf", [128, 128], "bfloat16"),
-    "c15": ("sbuf", [128, 128], "bfloat16"),
-    "ones": ("sbuf", [128, CH], "bfloat16"),
-    "r3": ("sbuf", [128, 8, 32], "bfloat16"),
-    "b3": ("sbuf", [128, 8, 32], "bfloat16"),
-    "bd": ("sbuf", [128, 8, 32], "bfloat16"),
-    "rot": ("sbuf", [128, 16, 8, 16], "bfloat16"),
+    "c12": ("sbuf", [128, CH], "bfloat16"),
+    "dg": ("sbuf", [128, 128], "bfloat16"),
+    "rq": ("sbuf", [128, 288], "bfloat16"),
     "j16": ("sbuf", [128, NT], "bfloat16"),
+    "jc": ("sbuf", [128, NT + 1], "bfloat16"),
     "nt": ("sbuf", [128, NT], "float32"),
     "nq0": ("sbuf", [128, NT], "float32"),
     "nq1": ("sbuf", [128, NT], "float32"),
-    "th16": ("sbuf", [128, 16], "float32"),
     "ecst": ("sbuf", [128, 10], "float32"),
-    "lmid": ("sbuf", [128, 4 * 28], "uint16"),
+    "skip": ("sbuf", [128, 20], "float32"),
+    "lmid": ("sbuf", [128, 4 * 32], "uint16"),
     "mk0": ("sbuf", [128, NT], "bfloat16"),
     "mk1": ("sbuf", [128, NT], "bfloat16"),
     "mk2": ("sbuf", [128, NT], "bfloat16"),
     "vld": ("sbuf", [128, NS], "bfloat16"),
     "cx": ("sbuf", [128, NT + 1], "bfloat16"),
     "cy": ("sbuf", [128, NT + 1], "bfloat16"),
+    "cz": ("sbuf", [128, NT + 1], "bfloat16"),
     "ai": ("sbuf", [128, NT], "int32"),
     "xf": ("sbuf", [128, NT], "bfloat16"),
     "tt": ("sbuf", [128, 15 * NT], "bfloat16"),
     "ap": ("sbuf", [128, NT + 1], "bfloat16"),
-    "aq": ("sbuf", [128, NT], "float32"),
-    "aq1": ("sbuf", [128, NT], "float32"),
     "sgn": ("sbuf", [128, 9 * NT], "bfloat16"),
     "acc": ("sbuf", [128, 10], "float32"),
+    "acs": ("sbuf", [128, 10], "float32"),
     "el": ("sbuf", [128, 10], "uint16"),
-    "flo": ("sbuf", [128, NT], "float32"),
-    "fhi": ("sbuf", [128, NT], "float32"),
-    "lh": ("sbuf", [128, LH1 + 2 * NS + 2], "float32"),
+    "flo": ("sbuf", [128, NT], "bfloat16"),
+    "fhi": ("sbuf", [128, NT], "bfloat16"),
+    "lo": ("sbuf", [128, NT + NS + 2], "float32"),
     "mx": ("sbuf", [128, NT + 1], "float32"),
     "lw": ("sbuf", [128, 144], "uint16"),
     "du": ("sbuf", [128, NT], "float32"),
     "dl0": ("sbuf", [128, NT], "uint16"),
     "dl1": ("sbuf", [128, NT], "uint16"),
-    "kt": ("sbuf", [128, 17], "float32"),
-    "et": ("sbuf", [128, 17], "float32"),
-    "eu": ("sbuf", [128, 17], "float32"),
-    "lpl": ("sbuf", [128, 18], "uint16"),
-    "ldy": ("sbuf", [128, 18], "uint16"),
+    "kq": ("sbuf", [128, 9], "float32"),
+    "kt": ("sbuf", [128, 9], "float32"),
+    "et": ("sbuf", [128, 9], "float32"),
+    "eu": ("sbuf", [128, 9], "float32"),
+    "lpl": ("sbuf", [128, 10], "uint16"),
+    "ldy": ("sbuf", [128, 10], "uint16"),
     "px": ("psum", [128, 512], "float32"),
     "py": ("psum", [128, 512], "float32"),
     "pz": ("psum", [128, 512], "float32"),
@@ -114,12 +120,19 @@ SCRATCH = {
     "pm2": ("psum", [128, 512], "float32"),
     "pm3": ("psum", [128, 512], "float32"),
 }
-SEMAPHORES = ["cV", "cS", "cP", "cG", "dxa", "dxb", "dv", "dw", "dst", "sent",
+SEMAPHORES = ["cV", "cS", "cP", "cG", "dxa", "dxb", "dv", "dt", "dg", "dw", "dst", "sent",
               "aE0", "aE1", "aC0", "aC1", "aR0", "aR1", "rC0", "rC1", "rR0", "rR1"]
 
 
 def n_eng(m):
     return bin(m).count("1")
+
+
+def engines_for(kind, t, src, dst, topo):
+    es = topo.engines(src, dst)
+    n, first = {"R": (ENG[0], 0), "C": (ENG[1 + t], 0), "E": (8, 1)}[kind]
+    step = max(1, len(es) // n)
+    return sum(1 << e for e in es[first % step::step])
 
 
 def far_rank(r, n):
@@ -150,14 +163,16 @@ def far_landing(T, t, r):
 def relay_program(g, core, T, topo, dst_rank):
     dst = T.cores[dst_rank]
     rid, pid = topo.addr(dst, core)
-    m = topo.mask(core, dst)
-    nin = n_eng(topo.mask(T.cores[far_rank(dst_rank, len(T.cores))], core))
+    src = T.cores[far_rank(dst_rank, len(T.cores))]
+    sent = 0
     for t in range(D):
-        g.wait_ge(T.sem["rR%d" % t], nin)
-        g.remote_dma(T["ri%d" % t][:, 0:1], T["ri%d" % t][:, 0:1], T.sem["aR%d" % t], T.sem.sent, pid, rid, m)
-        g.wait_ge(T.sem["rC%d" % t], nin)
-        g.remote_dma(far_landing(T, t, dst_rank), T["rl%d" % t][:], T.sem["aC%d" % t], T.sem.sent, pid, rid, m)
-    g.wait_ge(T.sem.sent, 2 * D * n_eng(m))
+        for kind, out, in_ in (("R", T["ri%d" % t][:, 0:2], T["ri%d" % t][:, 0:2]),
+                               ("C", far_landing(T, t, dst_rank), T["rl%d" % t][:])):
+            m = engines_for(kind, t, core, dst, topo)
+            g.wait_ge(T.sem["r%s%d" % (kind, t)], n_eng(engines_for(kind, t, src, core, topo)))
+            g.remote_dma(out, in_, T.sem["a%s%d" % (kind, t)], T.sem.sent, pid, rid, m)
+            sent += n_eng(m)
+    g.wait_ge(T.sem.sent, sent)
 
 
 def rank_program(g, core, T, topo):
@@ -175,6 +190,7 @@ def rank_program(g, core, T, topo):
     far = far_rank(r, n)
     near = r - 1 if odd else r + 1
     o16 = 0.0 if odd else 128.0
+    abf = 129.0 + 128.0 - o16
     LH, CV, MN, RH = layout(r)
     base = float(MN) + (0.0 if odd else CAP)
 
@@ -231,8 +247,8 @@ def rank_program(g, core, T, topo):
     def ms(ap, c, wk):
         op("V", lambda: g.vector.memset(ap, c), (), wk)
 
-    def scan(out, d0, d1, op0, rk, wk):
-        op("V", lambda: g.vector.tensor_tensor_scan(out, d0, d1, 0.0, op0, A.max), rk, wk)
+    def scan(out, d0, d1, op0, rk, wk, bk=()):
+        op("V", lambda: g.vector.tensor_tensor_scan(out, d0, d1, 0.0, op0, A.max), rk, wk, bk)
 
     def act(out, in_, f, rk, wk, bk=(), **kw):
         op("S", lambda: g.scalar.activation(out, in_, f, **kw), rk, wk, bk)
@@ -240,15 +256,15 @@ def rank_program(g, core, T, topo):
     def lin(out, in_, a, b, rk, wk, bk=()):
         act(out, in_, F.Identity, rk, wk, bk, scale=a, bias=b)
 
-    def sign(out, in_, a, b, rk, wk):
-        act(out, in_, F.Sign, rk, wk, scale=a, bias=b)
+    def sign(out, in_, a, b, rk, wk, bk=()):
+        act(out, in_, F.Sign, rk, wk, bk, scale=a, bias=b)
 
     def mm(out, lhsT, rhs, st, sp, rk, wk, bk):
         op("P", lambda: g.tensor.matmul(out, lhsT, rhs, st, sp), rk, wk, bk)
 
-    def iota(out, pat, cm, wk, fl=True):
+    def iota(out, pat, cm, wk, fl=True, base=0):
         if fl:
-            op("G", lambda: g.iota(out, pat, 0, cm, allow_small_or_imprecise_dtypes=True), (), wk)
+            op("G", lambda: g.iota(out, pat, base, cm, allow_small_or_imprecise_dtypes=True), (), wk)
         else:
             op("G", lambda: g.iota(out, pat, 0, cm), (), wk)
 
@@ -273,12 +289,12 @@ def rank_program(g, core, T, topo):
     def send(dst, out, in_, sem, rk):
         wait("G", deps("G", rk, (), ()))
         rid, pid = topo.addr(dst, core)
-        m = topo.mask(core, dst)
+        m = engines_for(sem[1], int(sem[2]), core, dst, topo)
         g.remote_dma(out, in_, T.sem[sem], T.sem.sent, pid, rid, m)
         sent[0] += n_eng(m)
 
-    names = ["i", "g", "ci", "q0", "q1", "f9", "c0", "th0", "th1", "th1p", "th1b", "d0", "d1", "s0", "s1", "i1",
-             "b0", "kk", "nk", "na", "cc", "dd", "dl", "lim", "h1", "h2"]
+    names = ["p", "g", "i", "q0", "q1", "f9", "c0", "th0", "th1", "d0", "d1", "th1p", "th1b", "s0", "s1", "u0", "u1",
+             "b0", "kk", "nk", "cc", "dd", "dl", "lim", "h1", "h2"]
 
     def C(k, w=1):
         j = names.index(k)
@@ -286,95 +302,129 @@ def rank_program(g, core, T, topo):
 
     g.sync.dma_start(T.xs[:, 0:XA], T.x[:, 0:XA]).then_inc(T.sem.dxa, 16)
     g.scalar.dma_start(T.vs[:], T.v[:]).then_inc(T.sem.dv, 16)
-    g.sync.dma_start(T.xs[:, XA:S], T.x[:, XA:S]).then_inc(T.sem.dxb, 16)
-    g.scalar.dma_start(T.ths[:], T.th[:]).then_inc(T.sem.dw, 16)
     g.scalar.dma_start(T.ws[:], T.w[:]).then_inc(T.sem.dw, 16)
-    g.scalar.dma_start(T.gps[:], T.gap[:]).then_inc(T.sem.dw, 16)
+    g.sync.dma_start(T.xs[:, XA:S], T.x[:, XA:S]).then_inc(T.sem.dxb, 16)
+    g.scalar.dma_start(T.ths[:], T.th[:]).then_inc(T.sem.dt, 16)
+    g.scalar.dma_start(T.gps[:], T.gap[:]).then_inc(T.sem.dg, 16)
     wr["xa"], wr["xb"], wr["vs"] = [("dxa", 16)], [("dxb", 16)], [("dv", 16)]
-    wr["ths"] = wr["ws"] = wr["gps"] = [("dw", 48)]
+    wr["ths"], wr["gps"] = [("dt", 16)], [("dg", 16)]
+    wr["ws"] = [("dw", 16)]
     for t in range(D):
-        wr["near%d" % t] = [("aE%d" % t, n_eng(topo.mask(cores[near], core)))]
+        wr["near%d" % t] = [("aE%d" % t, n_eng(engines_for("E", t, cores[near], core, topo)))]
         if far is not None:
             rl = relay_of(cores[far], core, cores, topo)
-            k = n_eng(topo.mask(cores[far] if rl is None else rl, core))
-            wr["far%d" % t], wr["ri%d" % t] = [("aC%d" % t, k)], [("aR%d" % t, k)]
+            for key, kind in (("far", "C"), ("ri", "R")):
+                k = n_eng(engines_for(kind, t, cores[far] if rl is None else rl, core, topo))
+                wr["%s%d" % (key, t)] = [("a%s%d" % (kind, t), k)]
 
     dconst = [8191.0 if odd else 8191.0 + CAP + 16, float(S + COV - 8193) if odd else 8191.0 + CAP - H]
+    NCS = [NT, NS]
+
+    def span_of(cuts, j):
+        a, b = cuts[j], cuts[j + 1]
+        return (a, b) if odd else (S - b, S - a)
+
+    PART = [span_of([0, TA, S], j) for j in range(2)]
+
+    def ycol(n):
+        early = PART[0][0] <= n < PART[0][1]
+        if odd:
+            return n + S - TA if early else n - TA
+        return NZ + (n - (S - TA) if early else n + TA)
+
+    def span(nc, k):
+        if k == 0:
+            return 0, nc
+        return (16 * k - 10, nc) if odd else (0, min(nc, nc + 16 * k - 123))
 
     iota(T.ki[:, 0:1], [[0, 1]], 1, ["ki0"], False)
     iota(T.g8[:], [[1, 8]], 0, ["g8"])
     iota(T.gm[:], [[1, 8], [0, 16]], 0, ["gm"])
-    iota(T.r3[:], [[-16, 8], [0, 2], [-1, 16]], 1, ["r3"])
     iota(T.j16[:], [[16, NT]], 0, ["j16"])
+    iota(T.dg[:], [[-1, 128]], 1, ["dg"])
     ms(T.sc[:], 0.0, ["sc0", "sc1"])
+    ms(T.c12[:], OFF, ["c12"])
     ts(T.ki[:, 1:2], T.ki[:, 0:1], 4, None, A.arith_shift_right, None, ["ki0"], ["ki1"])
     ts(T.ki[:, 2:3], T.ki[:, 0:1], 15, None, A.bitwise_and, None, ["ki0"], ["ki2"])
-    ms(T.ones[:], 1.0, ["ones"])
-    cp(C("g"), T.ki[:, 1:2], ["ki1"], ["g"])
-    cp(C("i"), T.ki[:, 2:3], ["ki2"], ["i"])
-    ms(T.c15[:], OFF / 128, ["c15"])
-    ts(T.neg16[:], T.gm[:], C("g"), -0.0625, A.is_equal, A.mult, ["gm", "g"], ["neg16"])
+    ms(T.rq[:], 0.0, ["rq0", "rq1", "rq2"])
+    cp(C("p", 3), T.ki[:, 0:3], ["ki0", "ki1", "ki2"], ["p", "g", "i"])
+    ms(T.cx[:, 0:1], 0.0, ["cx0"])
     ts(T.b8[:], T.g8[:], C("g"), None, A.is_equal, None, ["g8", "g"], ["b8"])
-    ts(T.b3[:], T.r3[:], 0.0, C("i"), A.is_equal, A.mult, ["r3", "i"], ["b3"])
+    ts(T.neg16[:], T.gm[:], C("g"), -0.0625, A.is_equal, A.mult, ["gm", "g"], ["neg16"])
     ts(T.one16[:], T.gm[:], C("g"), 0.0625, A.is_equal, A.mult, ["gm", "g"], ["one16"])
-    ts(T.sc[:, 15:143:16], T.b8[:], T.vs[:, 0:1], None, A.mult, None, ["b8", "vs"], ["sc0"])
-    tt(T.bd[:, :, 1:32], T.b3[:, :, 1:32], T.b3[:, :, 0:31], A.subtract, ["b3"], ["bd"])
+    for k, (a, c) in enumerate(((15, 1.0), (16, -1.0), (159, 1.0))):
+        ts(T.rq[:, a:a + 128:16], T.b8[:], C("i"), c / U, A.mult, A.mult, ["b8", "i"], ["rq%d" % k])
+    ms(T.jc[:, 0:1], -1.0, ["jc0"])
+    ts(C("f9"), C("i"), 9.0, None, A.is_lt, None, ["i"], ["f9"])
     ts(T.nt[:], T.j16[:], C("i"), None, A.add, None, ["j16", "i"], ["nt"])
+    ts(T.sc[:, 15:143:16], T.b8[:], T.vs[:, 0:1], None, A.mult, None, ["b8", "vs"], ["sc0"])
+    for k, c in (("idn", 1.0), ("idm", -1.0), ("idh", 0.5)):
+        ts(T[k][:], T.dg[:], 0.0, c, A.is_equal, A.mult, ["dg"], [k])
     sel(T.tm1[:], T.neg16[:], A.is_gt, 0.0, ["neg16"], ["tm1"])
-    sel(T.idn[:], T.ones[:, 0:128], A.is_equal, 0.0, ["ones"], ["idn"])
     sel(T.up16[:], T.tm1[:], A.not_equal, -512.0, ["tm1"], ["up16"])
-    for k in range(8, 15):
-        op("G", lambda: g.affine_select(T.rot[:, k], T.bd[:, :, 16 - k:32 - k], [[0, 8], [0, 16]], A.is_gt, 0.0, 1, 0),
-           ["bd"], ["rot%d" % k])
+    for t in range(D):
+        sk = [sum(span(NCS[t], k)) for k in range(9)]
+        n = 8 if sk[8] == sk[1] + 7 * (sk[2] - sk[1]) else 7
+        iota(T.skip[:, 10 * t + 1:10 * t + 1 + n], [[sk[2] - sk[1], n]], 0, ["ska%d" % t], base=sk[1])
+        iota(T.skip[:, 10 * t:10 * t + 9 - n // 8 * 8:8], [[0, 9 - n]], 0, ["skb%d" % t], base=sk[0])
     if odd:
         sel(T.up16b[:], T.tm1[:], A.not_equal, 512.0, ["tm1"], ["up16b"])
-    lin(T.b8s[:], T.b8[:], 0.125, 0.0, ["b8"], ["b8s"])
-    lin(C("ci"), C("i"), -0.0625, -0.0625 - 0.47, ["i"], ["ci"])
-    lin(C("i1"), C("i"), 0.0625, 0.0625, ["i"], ["i1"])
-    lin(C("q0"), C("i"), 0.0625, -129.0 - o16, ["i"], ["q0"])
-    lin(C("q1"), C("i"), 0.0625, -128.0 - o16, ["i"], ["q1"])
-    act(T.rot[:, 15], T.b3[:, :, 1:17], F.Copy, ["b3"], ["rot15"])
-    lin(T.th16[:], T.j16[:, 0:16], 1.0 / 256, C("i1"), ["j16", "i1"], ["th16"])
-    ms(T.cx[:, 0:1], 0.0, ["cx0"])
-    ms(T.lh[:, NT:LH1 + NS + 1:LH1 + NS - NT], 0.0, ["lhz"])
+    lin(C("q0"), C("i"), 0.0625, -129.0 - o16 + 1.0 / 32, ["i"], ["q0"])
+    lin(C("q1"), C("i"), -0.0625, 128.0 + o16 - 1.0 / 32, ["i"], ["q1"])
+    mm(T.pm3[:, 500:502], T.one16[:], T.vs[:], True, True, ["one16", "vs"], ["sumv"], ["pm3"])
+    lin(T.jc[:, 1:NT + 1], T.j16[:], 1.0 / U, -0.5, ["j16"], ["jc"])
+    lin(T.ecst[:], T.nt[:, 0:10], 1.0, -9.0 - o16 - 1.0 / 32, ["nt"], ["ecst"])
+    lin(C("th1p"), T.pm3[:, 501:502], 16 * OFF, BIG, ["sumv"], ["th1p"], ["pm3"])
+    lin(C("c0"), C("f9"), -119.0 - (8.0 if odd else 0.0), T.ecst[:, 0:1], ["f9", "ecst"], ["c0"])
+    lin(T.kq[:], T.nt[:, 0:9], 0.0625, base / 16 - 129.0 - o16 - (8.0 if odd else 0.0), ["nt"], ["kq"])
+    lin(T.nq0[:], T.nt[:], 0.0625, (NZ - dconst[0]) / 16, ["nt"], ["nq0"])
+    for k, (a, b) in enumerate(PART):
+        if a == b:
+            wr["nq2"] = []
+            continue
+        lin(T.nq1[:, a // 16:b // 16], T.nt[:, a // 16:b // 16], 0.0625, (ycol(a) - a - dconst[1]) / 16, ["nt"],
+            ["nq%d" % (k + 1)])
+    WM = ["wm%d" % k for k in range(8)]
+
+    def shift_lists(t):
+        for k in range(2 * t, 2 * t + 2):
+            ts(T.lmid[:, 32 * k:32 * k + 32], T.nt[:, 0:32], C("d%d" % t), 0.0 if k % 2 else float(H),
+               A.add if k % 2 else A.subtract, A.add, ["nt", "d%d" % t], ["lmid%d" % k])
+
+    ms(T.lo[:, NT:NT + 2 + NS:NS + 1], 0.0, ["loz"])
+    ts(T.sc[:, 159:287:16], T.b8[:], T.vs[:, 1:2], None, A.mult, None, ["b8", "vs"], ["sc1"])
+    ts(T.idb[:], T.dg[:], 0.0, BIG, A.is_equal, A.mult, ["dg"], ["idb"])
     for t in range(D):
         ms(T["w%d" % t][:, NW - 16:NW], 0.0, ["pad%d" % t])
         if far is None:
             ms(far_landing(T, t, r), 0.0, ["far%d" % t])
             ms(T["ri%d" % t][:], 0.0, ["ri%d" % t])
-    ts(C("f9"), C("i"), 9.0, None, A.is_lt, None, ["i"], ["f9"])
-    cp(C("th0", 2), T.ths[:], ["ths"], ["th0", "th1"])
-    cp(C("d0", 2), T.gps[:], ["gps"], ["d0", "d1"])
-    ts(T.sc[:, 159:287:16], T.b8[:], T.vs[:, 1:2], None, A.mult, None, ["b8", "vs"], ["sc1"])
+    ms(T.kc[:, 0:2], base / 16, ["kc0"])
+    ms(T.kc[:, 2:4], ((RH if odd else H) - base) / 16 + abf, ["kc"])
     for k in range(8):
-        act(T.wm[:, :, 16 * k:16 * k + 16], T.ws[:], F.Copy, ["ws", "b8s"], ["wm%d" % k], scale=T.b8s[:, k:k + 1])
-    WM = ["wm%d" % k for k in range(8)]
-    lin(T.ecst[:], T.nt[:, 0:10], 1.0, -9.0 - o16 - 1.0 / 32, ["nt"], ["ecst"])
-    for k in range(8):
-        act(T.rot[:, k], T.bd[:, :, 16 - k:32 - k], F.Copy, ["bd"], ["rot%d" % k])
-    lin(C("c0"), C("f9"), -119.0 - (8.0 if odd else 0.0), T.ecst[:, 0:1], ["f9", "ecst"], ["c0"])
-    lin(C("s0", 2), C("d0", 2), 1.0 if odd else -1.0, 0.0, ["d0", "d1"], ["sd"])
-    if odd:
-        lin(T.kt[:, 9:17], T.nt[:, 0:8], 1.0, 0.0, ["nt"], ["kts"])
-    else:
-        lin(T.kt[:, 0:8], T.nt[:, 0:8], 1.0, -128.0, ["nt"], ["kts"])
-    mm(T.pm3[:, 500:502], T.one16[:], T.vs[:], True, True, ["one16", "vs"], ["sumv"], ["pm3"])
-    lin(C("th1p"), T.pm3[:, 501:502], 16 * OFF, C("th1"), ["sumv", "th1"], ["th1p"], ["pm3"])
-    lin(T.nq0[:], T.nt[:], 0.0625, (NZ - dconst[0]) / 16, ["nt"], ["nq0"])
-    lin(T.idb[:], T.idn[:], BIG, 0.0, ["idn"], ["idb"])
-    lin(C("th1b"), C("th1p"), 1.0, BIG, ["th1p"], ["th1b"])
+        ts(T.wm[:, :, 16 * k:16 * k + 16], T.ws[:], T.b8[:, k:k + 1], 0.125, A.mult, A.mult, ["ws", "b8"], ["wm%d" % k])
 
     def offsets_mm(banks):
         for b, w in banks:
-            mm(T[b][:, 0:w], T.c15[:], T.ones[:, 0:w], True, False, ["c15", "ones"], [b], [b])
+            mm(T[b][:, 0:w], T.one16[:], T.c12[:, 0:w], True, False, ["one16", "c12"], [b], [b])
 
-    def scores(t, out, src, a, b, rk, flags=None):
+    def chw(t, i):
+        return CUM[t][i + 1] - CUM[t][i]
+
+    def cho(t, i):
+        return CUM[t][i] if odd else MID - CUM[t][i + 1]
+
+    def scores(t, o, src, a, b, rk, flags=None):
+        out = T.py[:, SC + o:SC + o + (b - a) // 16]
         if flags is not None:
-            mm(out, T.idb[:], flags[0], True, False, ["idb"] + flags[1], ["sco"], ["px"])
+            mm(out, T.idb[:], flags[0], True, False, ["idb"] + flags[1], ["sco"], ["py"])
         for i in range(16):
             u = 144 * t + 15 - i
             mm(out, T.sc[:, u:u + 128], src[:, a + i:b:16], i == 0 and flags is None, i == 15,
-               ["sc%d" % t] + rk, ["sco"], ["px"])
+               ["sc%d" % t] + rk, ["sco"], ["py"])
+
+    def keep(m, nc, th):
+        ts(T[m][:, 0:nc], T.py[:, SC:SC + nc], C(th), None, A.is_ge, None, ["sco", th], [m], ["py"])
 
     def prefix(nc, m, up):
         mk = T[m][:, 0:nc]
@@ -388,124 +438,146 @@ def rank_program(g, core, T, topo):
         return c, ck
 
     def ktc(a, b):
-        o = 0 if odd else 8
-        return T.kt[:, o + a:o + b]
+        return T.kt[:, a:b]
 
-    def lists(t, nc, s_after):
-        m = "mk%d" % t
-        mm(T.pz[:, 0:nc], T.idn[:], T.j16[:, 0:nc], True, False, ["idn", "j16"], ["rr"], ["pz"])
+    def lists(t, v_fill, s_after):
+        m, nc = "mk%d" % t, NCS[t]
+        rr = T.pz[:, 1:nc + 1]
+        mm(T.pz[:, 0:nc + 1], T.idn[:], T.jc[:, 0:nc + 1], True, False, ["idn", "jc", "jc0"], ["rr"], ["pz"])
         c, ck = prefix(nc, m, "up16")
+        if far is not None:
+            rl = relay_of(core, cores[far], cores, topo)
+            send(cores[far] if rl is None else rl, T["ri%d" % t][:, 0:2], T.cx[:, nc - 1:nc + 1],
+                 ("aR%d" if rl is None else "rR%d") % t, ["cx"])
         mm(T.py[:, 0:nc + 1], T.one16[:], c[:, 0:nc + 1], True, True, ["one16"] + ck, ["py"], ["py"])
-        mm(T.pe[:, 0:nc + 1], T.one16[:], c[:, 0:nc + 1], True, True, ["one16"] + ck, ["pe"], ["pe"])
-        mm(T.pz[:, 0:nc], T.rot[:, 15], T[m][:, 0:nc], False, False, ["rot15", m], ["rr"], ["pz"])
-        for k, o in ((0, A.subtract), (1, A.add)):
-            a = 56 * t + 28 * k
-            ts(T.lmid[:, a:a + 28], T.nt[:, 0:28], C("d%d" % t), 128.0, o, A.add, ["nt", "d%d" % t],
-               ["lmid%d%d" % (t, k)])
+        fb = ("pm3", "pe")
+        for k in (1, 0):
+            mm(T[fb[k]][:, 0:nc], T.one16[:], c[:, k:nc + k], True, False, ["one16"] + ck, [fb[k]], [fb[k]])
+        mm(rr, T.rq[:, 144:272], T[m][:, 0:nc], False, False, ["rq2", m], ["rr"], ["pz"])
         val = T.px[:, NT:NT + nc]
         kc = nc if odd else 0
-        ro, apk, pk = T["ro%d" % t][:, 0:1], T.ap[:, kc:kc + 1], T.py[:, kc:kc + 1]
+        apk, pk = T.ap[:, kc:kc + 1], T.py[:, kc:kc + 1]
         ab = 129.0 + o16
         act(T.ap[:, 0:nc + 1], T.py[:, 0:nc + 1], F.Identity, ["py"], ["ap"], ["py"], bias=ab - 0.47)
+        if t:
+            shift_lists(t)
+        else:
+            cp(C("d0", 2), T.gps[:], ["gps"], ["d0", "d1"])
+        for k in (1, 0):
+            mm(T[fb[k]][:, 0:nc], T.idm[:], T.ap[:, 0:nc], False, True, ["idm", "ap"], [fb[k]], [fb[k]])
 
         def count(k):
-            act(T.sgn[:, k * NT:k * NT + nc], T.py[:, 1:nc + 1], F.Sign, ["py", "ecst" if k else "b0"],
+            a, b = span(nc, k)
+            act(T.sgn[:, k * NT:k * NT + b - a], T.py[:, 1 + a:1 + b], F.Sign, ["py", "ecst" if k else "b0"],
                 ["acc%d" % k], ["py"], bias=T.ecst[:, k:k + 1] if k else C("b0"), scale=-1.0,
                 accum_out=T.acc[:, k:k + 1])
 
         count(1)
-        lin(C("na"), apk, -16.0, 16 * ab, ["ap"], ["na"])
         lin(C("b0"), apk, C("f9"), C("c0"), ["ap", "f9", "c0"], ["b0"])
-        lin(ro, pk, 16.0, C("na"), ["py", "na"], ["ro%d" % t], ["py"])
-        if far is not None:
-            rl = relay_of(core, cores[far], cores, topo)
-            send(cores[far] if rl is None else rl, T["ri%d" % t][:, 0:1], ro,
-                 ("aR%d" if rl is None else "rR%d") % t, ["ro%d" % t])
-        lin(T.aq[:, 0:nc], T.ap[:, 0:nc], 1.0, C("q0"), ["ap", "q0"], ["aq"])
-        lin(T.aq1[:, 0:nc], T.ap[:, 0:nc], 1.0, C("q1"), ["ap", "q1"], ["aq1"])
-        for k in (2, 3, 4, 5, 6, 7, 8, 0):
+        sign(T.fhi[:, 0:nc], T.pe[:, 0:nc], 1.0, C("q1"), ["pe", "q1"], ["fhi"], ["pe"])
+        for k in (2, 3, 4, 5, 6, 7):
             count(k)
+        sign(T.flo[:, 0:nc], T.pm3[:, 0:nc], -1.0, C("q0"), ["pm3", "q0"], ["flo"], ["pm3"])
+        count(8)
+        count(0)
+        if t == 0:
+            lin(C("u0", 2), C("d0", 2), 0.0625 if odd else -0.0625, 0.0, ["d0", "d1"], ["su"])
+            if not odd:
+                lin(C("s0", 2), C("d0", 2), -0.0625, COV / 16, ["d0", "d1"], ["sd"])
+        lin(T.kt[:], T.kq[:], 1.0, apk, ["kq", "ap"], ["kt"])
         cc = (-8.0 + (8193.0 / 16 if t else -8191.0 / 16)) if odd else 9.0 - 8191.0 / 16
         dd = (-1.0 if t else 128.0) if odd else (0.0 if t else -129.0)
-        lin(C("lim"), apk, 16.0, -16 * ab - (128.0 if odd else 0.0), ["ap"], ["lim"])
         lin(C("cc"), apk, 1.0, cc - ab, ["ap"], ["cc"])
         lin(C("dd"), apk, -1.0, dd + ab, ["ap"], ["dd"])
-        lin(ktc(0, 9), T.nt[:, 0:9], 1.0, C("lim"), ["nt", "lim"], ["ktc"])
-        lin(C("kk"), pk, 16.0, 0.0, ["py"], ["kk"], ["py"])
-        lin(C("nk"), pk, -16.0, (RH if odd else H) - base, ["py"], ["nk"], ["py"])
-        lin(T.et[:], T.kt[:], 1.0, C("s%d" % t), ["kts", "ktc", "sd"], ["et"])
-        s_after()
-
-        def slot_flags():
+        lin(T.et[:], T.kt[:], 1.0, C("u%d" % t), ["kt", "su"], ["et"])
+        if t == 0:
+            lin(C("th1b"), C("th1p"), 1.0, C("th1"), ["th1p", "th1"], ["th1b"])
             if odd:
                 lin(C("h1"), apk, 16.0, -16 * ab - 128.5, ["ap"], ["h1"])
-                lin(C("h2"), pk, 16.0, -0.5, ["py"], ["h2"], ["py"])
                 sign(T.vld[:, 0:120], T.nt[:, 0:120], -1.0, C("h1"), ["nt", "h1"], ["vla"])
-                sign(T.vld[:, 120:NS], ktc(0, 9), -1.0, C("h2"), ["ktc", "h2"], ["vlb", "vlc"])
             else:
                 lin(C("h1"), apk, -16.0, 16 * ab - CAP - COV + 0.5, ["ap"], ["h1"])
-                lin(C("h2"), pk, -16.0, 0.5, ["py"], ["h2"], ["py"])
-                sign(T.vld[:, 8:9], ktc(8, 9), -1.0, -0.5, ["ktc"], ["vlc"])
                 sign(T.vld[:, 9:NS], T.nt[:, 8:128], 1.0, C("h1"), ["nt", "h1"], ["vla"])
-                sign(T.vld[:, 0:8], ktc(0, 8), 1.0, C("h2"), ["ktc", "h2"], ["vlb"])
-            lin(T.nq1[:], T.nt[:], 0.0625, ((0 if odd else NZ) - dconst[1]) / 16, ["nt"], ["nq1"])
+        s_after()
 
-        ts(T.ai[:, 0:nc], val, C("ci"), -300.0, A.add, A.min, ["val", "ci"], ["ai"], ["px"])
+        ts(T.ai[:, 0:nc], val, -0.0625 - 0.47, -300.0, A.add, A.min, ["val"], ["ai"], ["px"])
         tt(T.xf[:, 0:nc], val, T.ai[:, 0:nc], A.subtract, ["val", "ai"], ["xf"], ["px"])
         for k in range(15):
             tk = T.tt[:, k * NT:k * NT + nc]
-            ts(tk, T.xf[:, 0:nc], T.th16[:, k:k + 1], None, A.is_le, None, ["xf", "th16"], ["t%d" % k])
-            mm(T.pz[:, 0:nc], T.rot[:, k], tk, False, k == 14, ["rot%d" % k, "t%d" % k], ["rr"], ["pz"])
-        tt(T.flo[:, 0:nc], T.pe[:, 0:nc], T.aq[:, 0:nc], A.is_le, ["pe", "aq"], ["flo"], ["pe"])
-        tt(T.fhi[:, 0:nc], T.pe[:, 1:nc + 1], T.aq1[:, 0:nc], A.is_gt, ["pe", "aq1"], ["fhi"], ["pe"])
-        b = LH1 * t
-        tt(T.lh[:, b:b + nc], T.pz[:, 0:nc], T.flo[:, 0:nc], A.mult, ["rr", "flo"], ["lo"], ["pz"])
-        tt(T.lh[:, b + nc + 1:b + 2 * nc + 1], T.pz[:, 0:nc], T.fhi[:, 0:nc], A.mult, ["rr", "fhi"], ["hi"], ["pz"])
-        ts(T.el[:, 0:9], T.acc[:, 0:9], float(nc), 0.5, A.add, A.mult, ["acc%d" % k for k in range(9)], ["el"])
-        scan(T.mx[:, 0:nc + 1], T.lh[:, b:b + nc + 1], T.lh[:, b + nc:b + 2 * nc + 1], A.max,
-             ["lo", "hi", "lhz"], ["mx"])
-        gather("V", T.lw[:], T.mx[:, 0:nc + 1], T.el[:, 0:9], 0, ["mx", "el"], ["lw"])
-        return slot_flags
+            ts(tk, T.xf[:, 0:nc], (k + 1) / 16.0, None, A.is_le, None, ["xf"], ["t%d" % k])
+            mm(rr, T.rq[:, 15 - k:143 - k], tk, False, k == 14, ["rq0", "rq1", "t%d" % k], ["rr"], ["pz"])
+            if k == FHI:
+                mm(rr, T.idh[:], T.fhi[:, 0:nc], False, False, ["idh", "fhi"], ["rr"], ["pz"])
+        ck2 = c[:, nc - 1:nc + 1] if odd else c[:, 0:2]
+        mm(T.px[:, 404:408], T.one16[:], T.kc[:], True, False, ["one16", "kc0", "kc"], ["kk"], ["px"])
+        mm(T.px[:, 404:406], T.one16[:], ck2, False, False, ck, ["kk"], ["px"])
+        mm(T.px[:, 406:408], T.neg16[:], ck2, False, True, ["neg16"] + ck, ["kk"], ["px"])
+        sk = ["ska%d" % t, "skb%d" % t]
+        v_fill()
+        a = (NT + 1) * t
+        tt(T.lo[:, a:a + nc], rr, T.flo[:, 0:nc], A.add, ["rr", "flo"], ["lo"], ["pz"])
+        tt(T.acs[:, 0:9], T.acc[:, 0:9], T.skip[:, 10 * t:10 * t + 9], A.add, ["acc%d" % k for k in range(9)] + sk,
+           ["acs"])
+        scan(T.mx[:, 0:nc + 1], T.lo[:, a:a + nc + 1], T.pz[:, 0:nc + 1], A.max, ["lo", "rr", "loz"], ["mx"], ["pz"])
+        ts(T.el[:, 0:9], T.acs[:, 0:9], 0.5, None, A.mult, None, ["acs"], ["el"])
+        ts(T.lw[:], T.mx[:, 0:nc + 1].indirect(T.el[:, 0:9]), U, None, A.mult, None, ["mx", "el"], ["lw"])
 
-    def fspan(j):
-        a, b = FCUT[j], FCUT[j + 1]
-        return (a, b) if odd else (S - b, S - a)
 
-    def place_list(t):
-        val, dw = T.px[:, NT:2 * NT], T.pz[:, 0:NT]
-        ts(T.du[:], val, C("cc"), C("dd"), A.is_ge if odd else A.is_lt, A.mult, ["val", "cc", "dd"], ["du"], ["px"])
-        tt(dw, val, T.du[:], A.add, ["val", "du"], ["rr"], ["px", "pz"])
-        tt(T.du[:], dw, T["nq%d" % t][:], A.max if odd and t else A.min, ["rr", "nq%d" % t], ["du"], ["pz"])
-        if odd or t == 0:
-            ts(T["dl%d" % t][:], T.du[:], 16.0, dconst[t], A.mult, A.add, ["du"], ["dl%d" % t])
-        else:
-            for c in range(4):
-                js = [j for j in range(len(FNEED)) if FNEED[j] == c]
-                a, b = fspan(js[-1])[0] // 16, fspan(js[0])[1] // 16
-                ts(T.dl1[:, a:b], T.du[:, a:b], 16.0, dconst[t] - CH * (3 - c), A.mult, A.add, ["du"], ["dl1%d" % c])
-            wr["dl1"] = wr["dl13"]
+    def weave(*chains):
+        for k in range(max(len(c) for c in chains)):
+            for c in chains:
+                if k < len(c):
+                    c[k]()
+
+    def place_list(t, a, b, outs):
+        val, dw, du, dl = T.px[:, NT + a:NT + b], T.px[:, a:b], T.du[:, a:b], T["dl%d" % t]
+        chain = [
+            lambda: ts(du, val, C("cc"), C("dd"), A.is_ge if odd else A.is_lt, A.mult, ["val", "cc", "dd"], ["du"],
+                       ["px"]),
+            lambda: tt(dw, val, du, A.add, ["val", "du"], ["dw"], ["px"]),
+            lambda: tt(du, dw, T["nq%d" % t][:, a:b], A.max if odd and t else A.min, ["dw", "nq%d" % t, "nq2"], ["du"],
+                       ["px"])]
+        for c, d, o in outs:
+            chain.append(lambda c=c, d=d, o=o: ts(dl[:, c:d], T.du[:, c:d], 16.0, dconst[t] - o, A.mult, A.add, ["du"],
+                                                  ["dl%d_%d" % (t, c)]))
+        return chain
 
     def plain_list(t):
-        ts(T.lpl[:, 0:17], T.kt[:], C("s%d" % t), base - (0 if odd else COV), A.subtract, A.add,
-           ["kts", "ktc", "sd"], ["lpl"])
+        ts(T.lpl[:, 0:9], T.kt[:], C(("u%d" if odd else "s%d") % t), 16.0, A.subtract, A.mult,
+           ["kt", "su" if odd else "sd"], ["lpl"])
+
+    kk, nk = (T.px[:, 405:406], T.px[:, 407:408]) if odd else (T.px[:, 404:405], T.px[:, 406:407])
 
     def far_list(t):
-        ts(C("dl"), T["ri%d" % t][:, 0:1], C("nk"), None, A.add, None, ["ri%d" % t, "nk"], ["dl"])
-        ts(T.eu[:], T.et[:], C("kk"), C("dl"), A.is_ge if odd else A.is_lt, A.mult, ["et", "kk", "dl"], ["eu"])
-        tt(T.eu[:], T.eu[:], T.et[:], A.add, ["et", "eu"], ["eu"])
-        ts(T.ldy[:, 0:17], T.eu[:], base, None, A.add, None, ["eu"], ["ldy"])
+        ri = T.px[:, 401:402]
+        return [
+            lambda: ts(T.apn[:, 0:1], ri, abf - 0.47, None, A.add, None, ["kf"], ["apn"], ["px"]),
+            lambda: ts(C("dl"), T.apn[:, 0:1], ri, nk, A.subtract, A.subtract, ["kf", "kk", "apn"], ["dl"], ["px"]),
+            lambda: ts(T.eu[:], T.et[:], kk, C("dl"), A.is_ge if odd else A.is_lt, A.mult, ["et", "kk", "dl"], ["eu"],
+                       ["px"]),
+            lambda: tt(T.eu[:], T.et[:], T.eu[:], A.subtract, ["et", "eu"], ["eu"]),
+            lambda: ts(T.ldy[:, 0:9], T.eu[:], 16.0, None, A.mult, None, ["eu"], ["ldy"])]
 
-    PIECE = [(8, 44), (44, 72), (72, 100), (100, 128)] if odd else [(84, 120), (56, 84), (28, 56), (0, 28)]
+    def slot_flags():
+        if odd:
+            return [lambda: ts(T.vld[:, 120:NS], T.kt[:], kk, None, A.is_lt, None, ["kt", "kk"], ["vlb", "vlc"], ["px"])]
+        return [
+            lambda: ts(T.vld[:, 0:8], T.kt[:, 0:8], kk, None, A.is_ge, None, ["kt", "kk"], ["vlb"], ["px"]),
+            lambda: ts(T.vld[:, 8:9], T.kt[:, 8:9], base / 16, None, A.is_lt, None, ["kt"], ["vlc"])]
 
-    def depth(t, src, sk, add, z, zmid, edge_out, plan, extra):
+    def piece(t, i):
+        a, b = (CUM[t][i] + H) // 16, (CUM[t][i + 1] + H) // 16
+        return (a, b) if odd else (128 - b, 128 - a)
+
+    def depth(t, src, sk, add, z, zmid, zcov, plan, extra):
         w = T["w%d" % t]
         wa, wb, wc = T.wm[:, 3 * t, :], T.wm[:, 3 * t + 1, :], T.wm[:, 3 * t + 2, :]
         K = lambda s: "%s%d" % (s, t)
         ea = 0 if odd else 120
         cov = w[:, CV:CV + COV]
-        offsets_mm([("pm%d" % c, CH) for c in (range(4) if t else [3])])
+        nch = len(CUM[t]) - 1
+        offsets_mm([(BANKS[i], chw(t, i)) for i in range(0 if t else 3, nch)] + [("pe", COV)])
         gather("V", cov, src, T.lw[:, 0:9], add, sk + ["lw"], [K("cov")])
-        offsets_mm([("pe", NE)])
         if far is not None:
             rl = relay_of(core, cores[far], cores, topo)
             if rl is None:
@@ -518,60 +590,61 @@ def rank_program(g, core, T, topo):
         na = nl[3] if odd else nl[0]
         send(cores[near], w[:, na:na + H], edge, K("aE"), [K("edg")])
         plain_list(t)
-        own = [K("c%d_" % j) for j in range(4)] + [K("edg"), K("cov"), K("near")]
-        epl, edy = ("xme", "xpe") if odd else ("xpe", "xme")
+        own = [K("c%d_" % j) for j in range(nch)] + [K("edg"), K("cov"), K("near")]
+        wn, wf = (wb, wc) if odd else (wc, wb)
 
         def task(e, name):
             kind = name[0]
-            if kind in "cmpMe":
+            if kind in "cmpAMe":
                 i = int(name[1])
-                c = i if odd else 3 - i
+                o, cw, b = cho(t, i), chw(t, i), BANKS[i]
+                a = MN + o + (0 if odd else H)
                 need = [K("c%d_" % i), K("c%d_" % (i - 1)) if i else K("edg")]
-                b = "pm%d" % i
             if kind == "c":
-                a, b = PIECE[i]
+                a, b = piece(t, i)
                 gather(e, w[:, MN + 16 * a:MN + 16 * b], src, T.lw[:, 10 + a:10 + b], add, sk + ["lw"],
                        [K("c%d_" % i)])
             elif kind in "mp":
-                a = MN + CH * c
-                k = 0 if kind == "m" else 1
-                gather(e, T["x" + kind][:, CH * i:CH * (i + 1)], w[:, a:a + CH + 2 * H],
-                       T.lmid[:, 56 * t + 28 * k:56 * t + 28 * k + 28], 0, need + ["lmid%d%d" % (t, k)], ["x" + name])
+                k = 0 if (kind == "m") == odd else 1
+                win = w[:, a:a + cw + H] if k else w[:, a - H:a + cw]
+                k += 2 * t
+                gather(e, T["x" + kind][:, o:o + cw], win, T.lmid[:, 32 * k:32 * k + cw // 16], 0,
+                       need + ["lmid%d" % k] + ([K("near")] if name == "m0" else []), ["x" + name])
+            elif kind == "A":
+                mm(T[b][:, 0:cw], wa, w[:, a:a + cw], False, False, WM + need, [b], [b])
+                mm(T[b][:, 0:cw], wf, T.xp[:, o:o + cw], False, False, ["xp%d" % i], [b], [b])
             elif kind == "M":
-                a = MN + H + CH * c
-                mm(T[b][:, 0:CH], wa, w[:, a:a + CH], False, False, WM + need, [b], [b])
-                mm(T[b][:, 0:CH], wb, T.xm[:, CH * i:CH * (i + 1)], False, False, ["xm%d" % i], [b], [b])
-                mm(T[b][:, 0:CH], wc, T.xp[:, CH * i:CH * (i + 1)], False, True, ["xp%d" % i], [b], [b])
+                mm(T[b][:, 0:cw], wn, T.xm[:, o:o + cw], False, True, ["xm%d" % i], [b], [b])
             elif kind == "e":
-                clip(z[:, zmid + CH * c:zmid + CH * (c + 1)], T[b][:, 0:CH], [K("zm%d_" % i)], b)
+                clip(z[:, zmid + o:zmid + o + cw], T[b][:, 0:cw], [K("zm%d_" % i)], b)
             elif name == "Es":
                 if odd:
-                    gather(e, T[epl][:], w[:, 0:RH], T.lpl[:, 0:17], 0, own + ["lpl"], [epl])
+                    gather(e, T.xme[:], w[:, 0:RH], T.lpl[:, 0:9], 0, own + ["lpl"], ["xme"])
                 else:
-                    gather(e, T[epl][:], w[:, COV:NW], T.lpl[:, 0:17], 0, own + [K("pad"), "lpl"], [epl])
+                    gather(e, T.xme[:], w[:, COV:NW], T.lpl[:, 0:9], 0, own + [K("pad"), "lpl"], ["xme"])
             elif name == "Ev":
-                gather(e, T[edy][:], w[:], T.ldy[:, 0:17], 0, own + [K("pad"), K("far"), "ldy"], [edy])
+                gather(e, T.xpe[:], w[:], T.ldy[:, 0:9], 0, own + [K("pad"), K("far"), "ldy"], ["xpe"])
             elif name == "EM":
-                p1, p2, e1 = (cov, edge, COV) if odd else (edge, cov, H)
-                mm(T.pe[:, 0:e1], wa, p1, False, False, WM + [K("edg"), K("cov")], ["pe"], ["pe"])
-                mm(T.pe[:, e1:NE], wa, p2, False, False, WM + [K("edg"), K("cov")], ["pe"], ["pe"])
-                mm(T.pe[:, 0:NE], wb if odd else wc, T[epl][:], False, False, [epl], ["pe"], ["pe"])
-                mm(T.pe[:, 0:NE], wc if odd else wb, T[edy][:], False, True, [edy], ["pe"], ["pe"])
+                mm(T.pe[:, 0:COV], wa, cov, False, False, WM + [K("cov")], ["pe"], ["pe"])
+                mm(T.pe[:, 0:COV], wn, T.xme[:], False, False, ["xme"], ["pe"], ["pe"])
+                mm(T.pe[:, 0:COV], wf, T.xpe[:], False, True, ["xpe"], ["pe"], ["pe"])
+            elif name == "x8":
+                s16 = "neg16" if odd else "one16"
+                mm(T.px[:, 400:402], T[s16][:], T[K("ri")][:, 0:2], True, True, [s16, K("ri")], ["kf"], ["px"])
             elif name == "Ee":
-                for j, (a, b, o) in enumerate(edge_out):
-                    clip(z[:, o:o + b - a], T.pe[:, a:b], [K("ze%d_" % j)], "pe")
-            elif name == "x2":
-                far_list(t)
+                clip(z[:, zcov:zcov + COV], T.pe[:, 0:COV], [K("ze")], "pe")
             else:
                 extra[name](e)
 
-        pre = {"Es": ["c0", "c1", "c2", "c3"], "Ev": ["c0", "c1", "c2", "c3", "x2"], "EM": ["Es", "Ev"],
-               "Ee": ["EM"]}
-        for i in range(4):
-            pre["m%d" % i] = pre["p%d" % i] = ["c%d" % j for j in range(max(0, i - 1), i + 1)]
-            pre["M%d" % i] = ["m%d" % i, "p%d" % i] + extra["preM"]
+        cs = ["c%d" % i for i in range(nch)]
+        pre = {"Es": cs, "Ev": cs + ["x2"], "EM": ["Es", "Ev"], "Ee": ["EM"]}
+        for i in range(nch):
+            pre["m%d" % i] = pre["p%d" % i] = cs[max(0, i - 1):i + 1]
+            pre["A%d" % i] = ["p%d" % i]
+            pre["M%d" % i] = ["m%d" % i, "A%d" % i]
             pre["e%d" % i] = ["M%d" % i]
         pre.update(extra["pre"])
+        pre["x2"] = pre.get("x2", []) + ["x8"]
         pend = {"V": list(plan[0]), "S": list(plan[1]), "P": list(plan[2])}
         done = set()
         while pend["V"] or pend["S"] or pend["P"]:
@@ -583,70 +656,119 @@ def rank_program(g, core, T, topo):
                     moved = True
             assert moved
 
-    offsets_mm([("pm%d" % c, CH) for c in range(3)])
-    scores(0, T.px[:, 0:XA // 16], T.xs, 0, XA, ["xa"])
-    ts(T.xz[:, NZ:NZ + XA], T.xs[:, 0:XA], OFF, None, A.add, None, ["xa"], ["x192a"])
-    scores(0, T.px[:, XA // 16:NT], T.xs, XA, S, ["xb"])
+    offsets_mm([(BANKS[i], chw(0, i)) for i in range(3)])
+    scores(0, 0, T.xs, 0, XA, ["xa"])
+    ts(T.xz[:, NZ + XS:NZ + XA], T.xs[:, XS:XA], OFF, None, A.add, None, ["xa"], ["x192a"])
+    lin(T.xz[:, NZ:NZ + XS], T.xs[:, 0:XS], 1.0, OFF, ["xa"], ["x192c"])
+    scores(0, XA // 16, T.xs, XA, S, ["xb"])
     ts(T.xz[:, NZ + XA:NZ + S], T.xs[:, XA:S], OFF, None, A.add, None, ["xb"], ["x192b"])
-    ts(T.mk0[:], T.px[:, 0:NT], C("th0"), None, A.is_ge, None, ["sco", "th0"], ["mk0"], ["px"])
-    flags = lists(0, NT, lambda: None)
-    zm = ["zm%d_0" % i for i in range(4)]
-    sa, sb = ((0, 64), (64, NS)) if odd else ((65, NS), (0, 65))
-    eo0 = [(COV, NE, 0), (0, COV, NZ - COV)] if odd else [(0, H, NZ - H), (H, NE, 0)]
+    cp(C("th0", 2), T.ths[:], ["ths"], ["th0", "th1"])
+    keep("mk0", NT, "th0")
+    lists(0, lambda: shift_lists(0), lambda: None)
+    es = ["e%d" % i for i in range(len(CUM[0]) - 1)]
+    zm = ["zm%d_0" % i for i in range(len(es))]
+    cut = [CUM[0][2] // 16, NS]
+    sa, sb = [(a, b) if odd else (NS - b, NS - a) for a, b in zip([0] + cut, cut)]
+    z0 = zm + ["ze0"]
 
     def slot_scores(ab, rk):
         a, b = ab
-        scores(1, T.px[:, a:b], T.xz, 16 * a, 16 * b, rk, (T.vld[:, a:b], ["vla", "vlb", "vlc"]))
+        scores(1, a, T.xz, 16 * a, 16 * b, rk, (T.vld[:, a:b], ["vla", "vlb", "vlc"]))
+
+    def expand(j):
+        def run(e):
+            a, b = span_of(YCUT, j)
+            o = ycol(a)
+            gather(e, T.yz[:, o:o + b - a], T.xz[:], T.dl0[:, a // 16:b // 16], 0,
+                   z0 + ["x192a", "x192b", "x192c", "dl0_0"], ["y1_%d" % j])
+        return run
 
     ex0 = {
-        "x1": lambda e: place_list(0),
-        "x3": lambda e: slot_scores(sa, zm[0:2] + ["ze0_0"]),
-        "x4": lambda e: slot_scores(sb, zm[2:4] + ["ze1_0"]),
-        "x5": lambda e: ts(T.mk1[:, 0:NS], T.px[:, 0:NS], C("th1b"), None, A.is_ge, None, ["sco", "th1b"], ["mk1"],
-                           ["px"]),
-        "x6": lambda e: flags(),
-        "pre": {"x3": ["e0", "e1", "Ee", "x1", "x6"], "x4": ["e2", "e3", "x3"], "x5": ["x4"]},
-        "preM": [],
+        "x1": lambda e: weave(place_list(0, 0, NT, [(0, NT, 0)]), slot_flags()),
+        "x2": lambda e: weave(far_list(0)),
+        "x3": lambda e: slot_scores(sa, zm[0:2]),
+        "x4": lambda e: slot_scores(sb, z0[2:]),
+        "x5": lambda e: keep("mk1", NS, "th1b"),
+        "y0": expand(0),
+        "y1": expand(1),
+        "pre": {"x3": es[0:2] + ["x1"], "x4": es[2:] + ["Ee", "x1"], "x5": ["x3", "x4", "x1"],
+                "y0": es + ["Ee", "x1"], "y1": es + ["Ee", "x1"]},
     }
-    depth(0, T.xs[:], ["xa", "xb"], 0, T.xz, H if odd else COV, eo0, PLAN0, ex0)
-    z0 = zm + ["ze0_0", "ze1_0"]
-    YB = 0 if odd else NZ
+    depth(0, T.xs[:], ["xa", "xb"], 0, T.xz, 0 if odd else COV, MID if odd else 0, PLAN0, ex0)
 
-    def expand(j, e):
-        a, b = YCUT[j], YCUT[j + 1]
-        gather(e, T.yz[:, YB + a:YB + b], T.xz[:], T.dl0[:, a // 16:b // 16], 0,
-               z0 + ["x192a", "x192b", "dl0"], ["y1_%d" % j])
+    lists(1, lambda: expand(2)("V"), lambda: expand(3)("S"))
+    ny = YCUT.index(TA)
+    ys = [["y1_%d" % j for j in range(ny)], ["y1_%d" % j for j in range(len(YCUT) - 1)]]
+    part_of = [0 if FCUT[j] < TA else 1 for j in range(len(FNEED))]
 
-    expand(0, "S")
+    def fwin(j):
+        c, late = FNEED[j], part_of[j]
+        if odd:
+            return 0 if late else S - TA, S + COV + CUM[1][c + 1]
+        return cho(1, c), NZ + (S if late else TA)
 
-    lists(1, NS, lambda: expand(1, "S"))
-    y1 = ["y1_%d" % j for j in range(4)]
+    def outs(k):
+        by = {}
+        for j in range(len(FNEED)):
+            if part_of[j] == k:
+                by.setdefault(fwin(j)[0], []).extend(span_of(FCUT, j))
+        return [(min(v) // 16, max(v) // 16, o) for o, v in by.items()]
 
     def final(j):
         def run(e):
-            a, b = fspan(j)
-            c = FNEED[j]
-            win = T.yz[:, 0:S + NE + CH * (c + 1)] if odd else T.yz[:, CH * (3 - c):NZ + S]
-            gather(e, T.ysb[:, a:b], win, T.dl1[:, a // 16:b // 16], -OFF,
-                   ["zm%d_1" % i for i in range(c + 1)] + ["ze0_1", "dl1"] + y1, ["ysb%d" % j])
+            a, b = span_of(FCUT, j)
+            c, d = fwin(j)
+            dl = ["dl1_%d" % x[0] for x in outs(part_of[j]) if x[2] == c]
+            gather(e, T.ysb[:, a:b], T.yz[:, c:d], T.dl1[:, a // 16:b // 16], -OFF,
+                   ["zm%d_1" % i for i in range(FNEED[j] + 1)] + ["ze1"] + dl + ys[part_of[j]], ["ysb%d" % j])
         return run
 
+    def token_scores(k):
+        a, b = PART[k]
+        scores(1, a // 16, T.yz, ycol(a), ycol(a) + b - a, ys[k], (T.mk0[:, a // 16:b // 16], ["mk0"]))
+
+    def token_places(k):
+        a, b = PART[k][0] // 16, PART[k][1] // 16
+        mk, val, cx = T.mk2[:, a:b], T.px[:, NT + a:NT + b], T.cz[:, 1 + a:1 + b]
+        up = "up16b" if odd else "up16"
+        ts(mk, T.py[:, SC + a:SC + b], C("th1b"), None, A.is_ge, None, ["sco", "th1b"], ["mk2"], ["py"])
+        mm(val, T[up][:], mk, True, False, [up, "mk2"], ["val"], ["px"])
+        init = T.cz[:, a:a + 1] if odd and k else 0.0
+        op("V", lambda: g.vector.tensor_tensor_scan(cx, mk, mk, init, A.add, A.max), ["mk2"] + ["cz"] * k, ["cz"])
+        if not odd:
+            cy = T.cy[:, 1 + a:1 + b]
+            if k:
+                ts(cy, cx, T.cz[:, b:b + 1], T.cz[:, NT:NT + 1], A.subtract, A.subtract, ["cz"], ["cy"])
+            else:
+                ts(cy, cx, T.cz[:, b:b + 1], None, A.subtract, None, ["cz"], ["cy"])
+            cx = cy
+        mm(val, T.one16[:], cx, False, True, ["one16", "cz" if odd else "cy"], ["val"], ["px"])
+
+    def before(x):
+        return PLAN1[2][:PLAN1[2].index(x)]
+
+    ca, cb = [(a // 16, b // 16) for a, b in PART]
     ex1 = {
-        "y2": lambda e: expand(2, e),
-        "y3": lambda e: expand(3, e),
-        "x1": lambda e: scores(1, T.px[:, 0:NT], T.yz, YB, YB + S, y1, (T.mk0[:], ["mk0"])),
-        "x3": lambda e: (ts(T.mk2[:], T.px[:, 0:NT], C("th1b"), None, A.is_ge, None, ["sco", "th1b"], ["mk2"], ["px"]),
-                         prefix(NT, "mk2", "up16b" if odd else "up16")),
-        "x4": lambda e: place_list(1),
-        "pre": {"x1": ["y2", "y3"], "x3": ["x1"], "x4": ["x3"]},
-        "preM": ["x3"],
+        "y4": expand(4),
+        "y5": expand(5),
+        "x1": lambda e: token_scores(0),
+        "x3": lambda e: token_places(0),
+        "x2": lambda e: weave(place_list(1, ca[0], ca[1], outs(0)), far_list(1)),
+        "z1": lambda e: token_scores(1),
+        "z3": lambda e: token_places(1),
+        "z2": lambda e: weave(place_list(1, cb[0], cb[1], outs(1))),
+        "x7": lambda e: None,
+        "z7": lambda e: None,
+        "pre": {"x3": before("x7") + ["x1"], "x7": ["x3"], "x2": ["x3"], "z1": ["y4", "y5", "x3"],
+                "x1": ["y%d" % j for j in range(4, ny)],
+                "z3": (before("z7") if TA < S else []) + ["z1", "x2"], "z7": ["z3"], "z2": ["z3"]},
     }
     for j in range(len(FNEED)):
         ex1["f%d" % j] = final(j)
-        ex1["pre"]["f%d" % j] = ["e%d" % i for i in range(FNEED[j] + 1)] + ["Ee", "x4"]
-    depth(1, T.xz[:, 0:NZ], z0, -OFF, T.yz, S + NE if odd else 0, [(0, NE, S if odd else MID)], PLAN1, ex1)
+        ex1["pre"]["f%d" % j] = ["e%d" % i for i in range(FNEED[j] + 1)] + ["Ee", "z2" if part_of[j] else "x2"]
+    depth(1, T.xz[:, 0:NZ], z0, -OFF, T.yz, S + COV if odd else 0, S if odd else MID, PLAN1, ex1)
     for js in STORES:
-        a, b = min(fspan(j)[0] for j in js), max(fspan(j)[1] for j in js)
+        a, b = min(span_of(FCUT, j)[0] for j in js), max(span_of(FCUT, j)[1] for j in js)
         wait("Y", deps("Y", ["ysb%d" % j for j in js], (), ()))
         g.sync.dma_start(T.y[:, a:b], T.ysb[:, a:b]).then_inc(T.sem.dst, 16)
     wait("G", [("c" + e, cnt[e]) for e in cnt] + [("sent", sent[0]), ("dst", 16 * len(STORES))])

from concourse.mybir import AluOpType, ActivationFunctionType

A = AluOpType
F = ActivationFunctionType

S, D, H, CAP = 2560, 2, 128, 2048
NT = S // 16
COV = H + 16
NZ = CAP + 16
NS = NZ // 16
MID = CAP - H
CUM = ([0, 512, 1024, 1536, MID], [0, 512, 1024, 1536, 1792, MID])
BANKS = ["pm0", "pm1", "pm2", "pm3", "pz"]
CH = 512
NW = 2 * COV + CAP + H + 16
OFF = 192.0
BIG = 65536.0
U = 8192.0
XA = 1536
FHI = 7
XS = 1280
ENG = (8, 8, 16)
SC = 256

PLAN0 = ("c1 c2 p1 m2 x1 e1 e2 x2 e0 e3 Ee y0 x5".split(),
         "c0 c3 m1 p2 p3 p0 m0 m3 Es Ev y1".split(),
         "A1 A2 M1 A3 M2 A0 x8 M0 M3 EM x3 x4".split())
PLAN1 = ("y4 c0 p1 m1 x3 m3 x2 e0 e1 Ee f0 f2 p4 e2 m4 e3 e4 f5 f7".split(),
         "y5 c1 c3 c2 p0 c4 m0 p3 p2 Es Ev m2 f1 f3 f4 f6".split(),
         "x1 A1 x8 x7 M1 A0 M0 A2 EM A3 M2 M3 A4 M4".split())
TA = 2560
YCUT = [0, 352, 1056, 1184, 1600, 2080, 2560]
FCUT = [0, 128, 256, 512, 1024, 1536, 1792, 2176, 2560]
FNEED = [0, 0, 0, 1, 2, 3, 4, 4]
STORES = [[0, 1], [2], [3], [4], [5], [6, 7]]

SCRATCH = {
    "xs": ("sbuf", [128, S], "bfloat16"),
    "xz": ("sbuf", [128, NZ + S], "bfloat16"),
    "yz": ("sbuf", [128, NZ + S], "bfloat16"),
    "w0": ("sbuf", [128, NW], "bfloat16"),
    "w1": ("sbuf", [128, NW], "bfloat16"),
    "xm": ("sbuf", [128, MID], "bfloat16"),
    "xp": ("sbuf", [128, MID], "bfloat16"),
    "xme": ("sbuf", [128, COV], "bfloat16"),
    "xpe": ("sbuf", [128, COV], "bfloat16"),
    "ysb": ("sbuf", [128, S], "float32"),
    "rl0": ("sbuf", [128, COV], "bfloat16"),
    "rl1": ("sbuf", [128, COV], "bfloat16"),
    "ri0": ("sbuf", [128, 8], "bfloat16"),
    "ri1": ("sbuf", [128, 8], "bfloat16"),
    "vs": ("sbuf", [128, 2], "bfloat16"),
    "ths": ("sbuf", [128, 2], "int32"),
    "gps": ("sbuf", [128, 2], "int32"),
    "apn": ("sbuf", [128, 2], "bfloat16"),
    "ws": ("sbuf", [128, 6, 16], "bfloat16"),
    "wm": ("sbuf", [128, 6, 128], "bfloat16"),
    "sc": ("sbuf", [128, 288], "bfloat16"),
    "ki": ("sbuf", [128, 4], "int32"),
    "col": ("sbuf", [128, 32], "float32"),
    "g8": ("sbuf", [128, 8], "float32"),
    "b8": ("sbuf", [128, 8], "float32"),
    "kc": ("sbuf", [128, 4], "bfloat16"),
    "gm": ("sbuf", [128, 128], "bfloat16"),
    "one16": ("sbuf", [128, 128], "bfloat16"),
    "neg16": ("sbuf", [128, 128], "bfloat16"),
    "up16": ("sbuf", [128, 128], "bfloat16"),
    "up16b": ("sbuf", [128, 128], "bfloat16"),
    "idn": ("sbuf", [128, 128], "bfloat16"),
    "idm": ("sbuf", [128, 128], "bfloat16"),
    "idh": ("sbuf", [128, 128], "bfloat16"),
    "idb": ("sbuf", [128, 128], "bfloat16"),
    "tm1": ("sbuf", [128, 128], "bfloat16"),
    "c12": ("sbuf", [128, CH], "bfloat16"),
    "dg": ("sbuf", [128, 128], "bfloat16"),
    "rq": ("sbuf", [128, 288], "bfloat16"),
    "j16": ("sbuf", [128, NT], "bfloat16"),
    "jc": ("sbuf", [128, NT + 1], "bfloat16"),
    "nt": ("sbuf", [128, NT], "float32"),
    "nq0": ("sbuf", [128, NT], "float32"),
    "nq1": ("sbuf", [128, NT], "float32"),
    "ecst": ("sbuf", [128, 10], "float32"),
    "skip": ("sbuf", [128, 20], "float32"),
    "lmid": ("sbuf", [128, 4 * 32], "uint16"),
    "mk0": ("sbuf", [128, NT], "bfloat16"),
    "mk1": ("sbuf", [128, NT], "bfloat16"),
    "mk2": ("sbuf", [128, NT], "bfloat16"),
    "vld": ("sbuf", [128, NS], "bfloat16"),
    "cx": ("sbuf", [128, NT + 1], "bfloat16"),
    "cy": ("sbuf", [128, NT + 1], "bfloat16"),
    "cz": ("sbuf", [128, NT + 1], "bfloat16"),
    "ai": ("sbuf", [128, NT], "int32"),
    "xf": ("sbuf", [128, NT], "bfloat16"),
    "tt": ("sbuf", [128, 15 * NT], "bfloat16"),
    "ap": ("sbuf", [128, NT + 1], "bfloat16"),
    "sgn": ("sbuf", [128, 9 * NT], "bfloat16"),
    "acc": ("sbuf", [128, 10], "float32"),
    "acs": ("sbuf", [128, 10], "float32"),
    "el": ("sbuf", [128, 10], "uint16"),
    "flo": ("sbuf", [128, NT], "bfloat16"),
    "fhi": ("sbuf", [128, NT], "bfloat16"),
    "lo": ("sbuf", [128, NT + NS + 2], "float32"),
    "mx": ("sbuf", [128, NT + 1], "float32"),
    "lw": ("sbuf", [128, 144], "uint16"),
    "du": ("sbuf", [128, NT], "float32"),
    "dl0": ("sbuf", [128, NT], "uint16"),
    "dl1": ("sbuf", [128, NT], "uint16"),
    "kq": ("sbuf", [128, 9], "float32"),
    "kt": ("sbuf", [128, 9], "float32"),
    "et": ("sbuf", [128, 9], "float32"),
    "eu": ("sbuf", [128, 9], "float32"),
    "lpl": ("sbuf", [128, 10], "uint16"),
    "ldy": ("sbuf", [128, 10], "uint16"),
    "px": ("psum", [128, 512], "float32"),
    "py": ("psum", [128, 512], "float32"),
    "pz": ("psum", [128, 512], "float32"),
    "pe": ("psum", [128, 512], "float32"),
    "pm0": ("psum", [128, 512], "float32"),
    "pm1": ("psum", [128, 512], "float32"),
    "pm2": ("psum", [128, 512], "float32"),
    "pm3": ("psum", [128, 512], "float32"),
}
SEMAPHORES = ["cV", "cS", "cP", "cG", "dxa", "dxb", "dv", "dt", "dg", "dw", "dst", "sent",
              "aE0", "aE1", "aC0", "aC1", "aR0", "aR1", "rC0", "rC1", "rR0", "rR1"]


def n_eng(m):
    return bin(m).count("1")


def engines_for(kind, t, src, dst, topo):
    es = topo.engines(src, dst)
    n, first = {"R": (ENG[0], 0), "C": (ENG[1 + t], 0), "E": (8, 1)}[kind]
    step = max(1, len(es) // n)
    return sum(1 << e for e in es[first % step::step])


def far_rank(r, n):
    f = r + 1 if r % 2 else r - 1
    return f if 0 <= f < n else None


def relay_of(src, dst, cores, topo):
    if topo.may_write(src, dst):
        return None
    c = [k for k in topo.cores_of(src) if k not in cores and topo.may_write(k, dst)]
    c.sort(key=lambda k: topo.die(k) != topo.die(src))
    return c[0]


def layout(r):
    if r % 2:
        return 0, H + CAP, H, H + CAP + COV
    return 0, COV, 2 * COV, 2 * COV + CAP


def far_landing(T, t, r):
    lh, _, _, rh = layout(r)
    a = rh if r % 2 else lh
    return T["w%d" % t][:, a:a + COV]


def relay_program(g, core, T, topo, dst_rank):
    dst = T.cores[dst_rank]
    rid, pid = topo.addr(dst, core)
    src = T.cores[far_rank(dst_rank, len(T.cores))]
    sent = 0
    for t in range(D):
        for kind, out, in_ in (("R", T["ri%d" % t][:, 0:2], T["ri%d" % t][:, 0:2]),
                               ("C", far_landing(T, t, dst_rank), T["rl%d" % t][:])):
            m = engines_for(kind, t, core, dst, topo)
            g.wait_ge(T.sem["r%s%d" % (kind, t)], n_eng(engines_for(kind, t, src, core, topo)))
            g.remote_dma(out, in_, T.sem["a%s%d" % (kind, t)], T.sem.sent, pid, rid, m)
            sent += n_eng(m)
    g.wait_ge(T.sem.sent, sent)


def rank_program(g, core, T, topo):
    cores = list(T.cores)
    n = len(cores)
    r = T.rank_of(core)
    if r is None:
        for k in range(n):
            f = far_rank(k, n)
            if f is not None and relay_of(cores[k], cores[f], cores, topo) == core:
                relay_program(g, core, T, topo, f)
        return

    odd = r % 2 == 1
    far = far_rank(r, n)
    near = r - 1 if odd else r + 1
    o16 = 0.0 if odd else 128.0
    abf = 129.0 + 128.0 - o16
    LH, CV, MN, RH = layout(r)
    base = float(MN) + (0.0 if odd else CAP)

    eng = {"V": g.vector, "S": g.scalar, "P": g.tensor, "G": g, "Y": g.sync}
    cnt = {"V": 0, "S": 0, "P": 0, "G": 0}
    seen = {e: {} for e in eng}
    wr, rd, bank = {}, {}, {}
    sent = [0]

    def wait(e, toks):
        need = {}
        for s, v in toks:
            need[s] = max(need.get(s, 0), v)
        for s, v in need.items():
            if seen[e].get(s, 0) < v:
                eng[e].wait_ge(T.sem[s], v)
                seen[e][s] = v

    def deps(e, rk, wk, bk):
        toks = []
        for k in rk:
            toks += wr[k]
        for k in wk:
            toks += [x for x in wr.get(k, []) + rd.get(k, []) if not (e == "P" and x[0] == "cP")]
        for k in bk:
            toks += [(s, v) for s, v in bank.get(k, {}).items() if s != "c" + e]
        return toks

    def op(e, call, rk=(), wk=(), bk=()):
        wait(e, deps(e, rk, wk, bk))
        cnt[e] += 1
        call().then_inc(T.sem["c" + e], 1)
        tok = ("c" + e, cnt[e])
        for k in rk:
            rd.setdefault(k, []).append(tok)
        for k in wk:
            wr[k] = [tok]
            rd[k] = []
        for k in bk:
            bank.setdefault(k, {})[tok[0]] = tok[1]

    def ts(out, in0, s1, s2, op0, op1, rk, wk, bk=()):
        if op1 is None:
            op("V", lambda: g.vector.tensor_scalar(out, in0, s1, None, op0), rk, wk, bk)
        else:
            op("V", lambda: g.vector.tensor_scalar(out, in0, s1, s2, op0, op1), rk, wk, bk)

    def tt(out, in0, in1, o, rk, wk, bk=()):
        op("V", lambda: g.vector.tensor_tensor(out, in0, in1, o), rk, wk, bk)

    def cp(out, in_, rk, wk, bk=()):
        op("V", lambda: g.vector.tensor_copy(out, in_), rk, wk, bk)

    def ms(ap, c, wk):
        op("V", lambda: g.vector.memset(ap, c), (), wk)

    def scan(out, d0, d1, op0, rk, wk, bk=()):
        op("V", lambda: g.vector.tensor_tensor_scan(out, d0, d1, 0.0, op0, A.max), rk, wk, bk)

    def act(out, in_, f, rk, wk, bk=(), **kw):
        op("S", lambda: g.scalar.activation(out, in_, f, **kw), rk, wk, bk)

    def lin(out, in_, a, b, rk, wk, bk=()):
        act(out, in_, F.Identity, rk, wk, bk, scale=a, bias=b)

    def sign(out, in_, a, b, rk, wk, bk=()):
        act(out, in_, F.Sign, rk, wk, bk, scale=a, bias=b)

    def mm(out, lhsT, rhs, st, sp, rk, wk, bk):
        op("P", lambda: g.tensor.matmul(out, lhsT, rhs, st, sp), rk, wk, bk)

    def iota(out, pat, cm, wk, fl=True, base=0):
        if fl:
            op("G", lambda: g.iota(out, pat, base, cm, allow_small_or_imprecise_dtypes=True), (), wk)
        else:
            op("G", lambda: g.iota(out, pat, 0, cm), (), wk)

    def sel(out, in_, cmp, fill, rk, wk):
        op("G", lambda: g.affine_select(out, in_, [[-1, 128]], cmp, fill, 0, 1), rk, wk)

    def gather(e, out, win, lst, add, rk, wk):
        src = win.indirect(lst)
        if e == "V":
            if add:
                ts(out, src, add, None, A.add, None, rk, wk)
            else:
                cp(out, src, rk, wk)
        elif add:
            act(out, src, F.Identity, rk, wk, bias=add)
        else:
            act(out, src, F.Copy, rk, wk)

    def clip(out, in_, wk, b):
        ts(out, in_, OFF + 15, OFF - 15, A.min, A.max, [b], wk, [b])

    def send(dst, out, in_, sem, rk):
        wait("G", deps("G", rk, (), ()))
        rid, pid = topo.addr(dst, core)
        m = engines_for(sem[1], int(sem[2]), core, dst, topo)
        g.remote_dma(out, in_, T.sem[sem], T.sem.sent, pid, rid, m)
        sent[0] += n_eng(m)

    names = ["p", "g", "i", "q0", "q1", "f9", "c0", "th0", "th1", "d0", "d1", "th1p", "th1b", "s0", "s1", "u0", "u1",
             "b0", "kk", "nk", "cc", "dd", "dl", "lim", "h1", "h2"]

    def C(k, w=1):
        j = names.index(k)
        return T.col[:, j:j + w]

    g.sync.dma_start(T.xs[:, 0:XA], T.x[:, 0:XA]).then_inc(T.sem.dxa, 16)
    g.scalar.dma_start(T.vs[:], T.v[:]).then_inc(T.sem.dv, 16)
    g.scalar.dma_start(T.ws[:], T.w[:]).then_inc(T.sem.dw, 16)
    g.sync.dma_start(T.xs[:, XA:S], T.x[:, XA:S]).then_inc(T.sem.dxb, 16)
    g.scalar.dma_start(T.ths[:], T.th[:]).then_inc(T.sem.dt, 16)
    g.scalar.dma_start(T.gps[:], T.gap[:]).then_inc(T.sem.dg, 16)
    wr["xa"], wr["xb"], wr["vs"] = [("dxa", 16)], [("dxb", 16)], [("dv", 16)]
    wr["ths"], wr["gps"] = [("dt", 16)], [("dg", 16)]
    wr["ws"] = [("dw", 16)]
    for t in range(D):
        wr["near%d" % t] = [("aE%d" % t, n_eng(engines_for("E", t, cores[near], core, topo)))]
        if far is not None:
            rl = relay_of(cores[far], core, cores, topo)
            for key, kind in (("far", "C"), ("ri", "R")):
                k = n_eng(engines_for(kind, t, cores[far] if rl is None else rl, core, topo))
                wr["%s%d" % (key, t)] = [("a%s%d" % (kind, t), k)]

    dconst = [8191.0 if odd else 8191.0 + CAP + 16, float(S + COV - 8193) if odd else 8191.0 + CAP - H]
    NCS = [NT, NS]

    def span_of(cuts, j):
        a, b = cuts[j], cuts[j + 1]
        return (a, b) if odd else (S - b, S - a)

    PART = [span_of([0, TA, S], j) for j in range(2)]

    def ycol(n):
        early = PART[0][0] <= n < PART[0][1]
        if odd:
            return n + S - TA if early else n - TA
        return NZ + (n - (S - TA) if early else n + TA)

    def span(nc, k):
        if k == 0:
            return 0, nc
        return (16 * k - 10, nc) if odd else (0, min(nc, nc + 16 * k - 123))

    iota(T.ki[:, 0:1], [[0, 1]], 1, ["ki0"], False)
    iota(T.g8[:], [[1, 8]], 0, ["g8"])
    iota(T.gm[:], [[1, 8], [0, 16]], 0, ["gm"])
    iota(T.j16[:], [[16, NT]], 0, ["j16"])
    iota(T.dg[:], [[-1, 128]], 1, ["dg"])
    ms(T.sc[:], 0.0, ["sc0", "sc1"])
    ms(T.c12[:], OFF, ["c12"])
    ts(T.ki[:, 1:2], T.ki[:, 0:1], 4, None, A.arith_shift_right, None, ["ki0"], ["ki1"])
    ts(T.ki[:, 2:3], T.ki[:, 0:1], 15, None, A.bitwise_and, None, ["ki0"], ["ki2"])
    ms(T.rq[:], 0.0, ["rq0", "rq1", "rq2"])
    cp(C("p", 3), T.ki[:, 0:3], ["ki0", "ki1", "ki2"], ["p", "g", "i"])
    ms(T.cx[:, 0:1], 0.0, ["cx0"])
    ts(T.b8[:], T.g8[:], C("g"), None, A.is_equal, None, ["g8", "g"], ["b8"])
    ts(T.neg16[:], T.gm[:], C("g"), -0.0625, A.is_equal, A.mult, ["gm", "g"], ["neg16"])
    ts(T.one16[:], T.gm[:], C("g"), 0.0625, A.is_equal, A.mult, ["gm", "g"], ["one16"])
    for k, (a, c) in enumerate(((15, 1.0), (16, -1.0), (159, 1.0))):
        ts(T.rq[:, a:a + 128:16], T.b8[:], C("i"), c / U, A.mult, A.mult, ["b8", "i"], ["rq%d" % k])
    ms(T.jc[:, 0:1], -1.0, ["jc0"])
    ts(C("f9"), C("i"), 9.0, None, A.is_lt, None, ["i"], ["f9"])
    ts(T.nt[:], T.j16[:], C("i"), None, A.add, None, ["j16", "i"], ["nt"])
    ts(T.sc[:, 15:143:16], T.b8[:], T.vs[:, 0:1], None, A.mult, None, ["b8", "vs"], ["sc0"])
    for k, c in (("idn", 1.0), ("idm", -1.0), ("idh", 0.5)):
        ts(T[k][:], T.dg[:], 0.0, c, A.is_equal, A.mult, ["dg"], [k])
    sel(T.tm1[:], T.neg16[:], A.is_gt, 0.0, ["neg16"], ["tm1"])
    sel(T.up16[:], T.tm1[:], A.not_equal, -512.0, ["tm1"], ["up16"])
    for t in range(D):
        sk = [sum(span(NCS[t], k)) for k in range(9)]
        n = 8 if sk[8] == sk[1] + 7 * (sk[2] - sk[1]) else 7
        iota(T.skip[:, 10 * t + 1:10 * t + 1 + n], [[sk[2] - sk[1], n]], 0, ["ska%d" % t], base=sk[1])
        iota(T.skip[:, 10 * t:10 * t + 9 - n // 8 * 8:8], [[0, 9 - n]], 0, ["skb%d" % t], base=sk[0])
    if odd:
        sel(T.up16b[:], T.tm1[:], A.not_equal, 512.0, ["tm1"], ["up16b"])
    lin(C("q0"), C("i"), 0.0625, -129.0 - o16 + 1.0 / 32, ["i"], ["q0"])
    lin(C("q1"), C("i"), -0.0625, 128.0 + o16 - 1.0 / 32, ["i"], ["q1"])
    mm(T.pm3[:, 500:502], T.one16[:], T.vs[:], True, True, ["one16", "vs"], ["sumv"], ["pm3"])
    lin(T.jc[:, 1:NT + 1], T.j16[:], 1.0 / U, -0.5, ["j16"], ["jc"])
    lin(T.ecst[:], T.nt[:, 0:10], 1.0, -9.0 - o16 - 1.0 / 32, ["nt"], ["ecst"])
    lin(C("th1p"), T.pm3[:, 501:502], 16 * OFF, BIG, ["sumv"], ["th1p"], ["pm3"])
    lin(C("c0"), C("f9"), -119.0 - (8.0 if odd else 0.0), T.ecst[:, 0:1], ["f9", "ecst"], ["c0"])
    lin(T.kq[:], T.nt[:, 0:9], 0.0625, base / 16 - 129.0 - o16 - (8.0 if odd else 0.0), ["nt"], ["kq"])
    lin(T.nq0[:], T.nt[:], 0.0625, (NZ - dconst[0]) / 16, ["nt"], ["nq0"])
    for k, (a, b) in enumerate(PART):
        if a == b:
            wr["nq2"] = []
            continue
        lin(T.nq1[:, a // 16:b // 16], T.nt[:, a // 16:b // 16], 0.0625, (ycol(a) - a - dconst[1]) / 16, ["nt"],
            ["nq%d" % (k + 1)])
    WM = ["wm%d" % k for k in range(8)]

    def shift_lists(t):
        for k in range(2 * t, 2 * t + 2):
            ts(T.lmid[:, 32 * k:32 * k + 32], T.nt[:, 0:32], C("d%d" % t), 0.0 if k % 2 else float(H),
               A.add if k % 2 else A.subtract, A.add, ["nt", "d%d" % t], ["lmid%d" % k])

    ms(T.lo[:, NT:NT + 2 + NS:NS + 1], 0.0, ["loz"])
    ts(T.sc[:, 159:287:16], T.b8[:], T.vs[:, 1:2], None, A.mult, None, ["b8", "vs"], ["sc1"])
    ts(T.idb[:], T.dg[:], 0.0, BIG, A.is_equal, A.mult, ["dg"], ["idb"])
    for t in range(D):
        ms(T["w%d" % t][:, NW - 16:NW], 0.0, ["pad%d" % t])
        if far is None:
            ms(far_landing(T, t, r), 0.0, ["far%d" % t])
            ms(T["ri%d" % t][:], 0.0, ["ri%d" % t])
    ms(T.kc[:, 0:2], base / 16, ["kc0"])
    ms(T.kc[:, 2:4], ((RH if odd else H) - base) / 16 + abf, ["kc"])
    for k in range(8):
        ts(T.wm[:, :, 16 * k:16 * k + 16], T.ws[:], T.b8[:, k:k + 1], 0.125, A.mult, A.mult, ["ws", "b8"], ["wm%d" % k])

    def offsets_mm(banks):
        for b, w in banks:
            mm(T[b][:, 0:w], T.one16[:], T.c12[:, 0:w], True, False, ["one16", "c12"], [b], [b])

    def chw(t, i):
        return CUM[t][i + 1] - CUM[t][i]

    def cho(t, i):
        return CUM[t][i] if odd else MID - CUM[t][i + 1]

    def scores(t, o, src, a, b, rk, flags=None):
        out = T.py[:, SC + o:SC + o + (b - a) // 16]
        if flags is not None:
            mm(out, T.idb[:], flags[0], True, False, ["idb"] + flags[1], ["sco"], ["py"])
        for i in range(16):
            u = 144 * t + 15 - i
            mm(out, T.sc[:, u:u + 128], src[:, a + i:b:16], i == 0 and flags is None, i == 15,
               ["sc%d" % t] + rk, ["sco"], ["py"])

    def keep(m, nc, th):
        ts(T[m][:, 0:nc], T.py[:, SC:SC + nc], C(th), None, A.is_ge, None, ["sco", th], [m], ["py"])

    def prefix(nc, m, up):
        mk = T[m][:, 0:nc]
        mm(T.px[:, NT:NT + nc], T[up][:], mk, True, False, [up, m], ["val"], ["px"])
        scan(T.cx[:, 1:nc + 1], mk, mk, A.add, [m], ["cx"])
        c, ck = T.cx, ["cx", "cx0"]
        if not odd:
            ts(T.cy[:, 0:nc + 1], T.cx[:, 0:nc + 1], T.cx[:, nc:nc + 1], None, A.subtract, None, ck, ["cy"])
            c, ck = T.cy, ["cy"]
        mm(T.px[:, NT:NT + nc], T.one16[:], c[:, 1:nc + 1], False, True, ["one16"] + ck, ["val"], ["px"])
        return c, ck

    def ktc(a, b):
        return T.kt[:, a:b]

    def lists(t, v_fill, s_after):
        m, nc = "mk%d" % t, NCS[t]
        rr = T.pz[:, 1:nc + 1]
        mm(T.pz[:, 0:nc + 1], T.idn[:], T.jc[:, 0:nc + 1], True, False, ["idn", "jc", "jc0"], ["rr"], ["pz"])
        c, ck = prefix(nc, m, "up16")
        if far is not None:
            rl = relay_of(core, cores[far], cores, topo)
            send(cores[far] if rl is None else rl, T["ri%d" % t][:, 0:2], T.cx[:, nc - 1:nc + 1],
                 ("aR%d" if rl is None else "rR%d") % t, ["cx"])
        mm(T.py[:, 0:nc + 1], T.one16[:], c[:, 0:nc + 1], True, True, ["one16"] + ck, ["py"], ["py"])
        fb = ("pm3", "pe")
        for k in (1, 0):
            mm(T[fb[k]][:, 0:nc], T.one16[:], c[:, k:nc + k], True, False, ["one16"] + ck, [fb[k]], [fb[k]])
        mm(rr, T.rq[:, 144:272], T[m][:, 0:nc], False, False, ["rq2", m], ["rr"], ["pz"])
        val = T.px[:, NT:NT + nc]
        kc = nc if odd else 0
        apk, pk = T.ap[:, kc:kc + 1], T.py[:, kc:kc + 1]
        ab = 129.0 + o16
        act(T.ap[:, 0:nc + 1], T.py[:, 0:nc + 1], F.Identity, ["py"], ["ap"], ["py"], bias=ab - 0.47)
        if t:
            shift_lists(t)
        else:
            cp(C("d0", 2), T.gps[:], ["gps"], ["d0", "d1"])
        for k in (1, 0):
            mm(T[fb[k]][:, 0:nc], T.idm[:], T.ap[:, 0:nc], False, True, ["idm", "ap"], [fb[k]], [fb[k]])

        def count(k):
            a, b = span(nc, k)
            act(T.sgn[:, k * NT:k * NT + b - a], T.py[:, 1 + a:1 + b], F.Sign, ["py", "ecst" if k else "b0"],
                ["acc%d" % k], ["py"], bias=T.ecst[:, k:k + 1] if k else C("b0"), scale=-1.0,
                accum_out=T.acc[:, k:k + 1])

        count(1)
        lin(C("b0"), apk, C("f9"), C("c0"), ["ap", "f9", "c0"], ["b0"])
        sign(T.fhi[:, 0:nc], T.pe[:, 0:nc], 1.0, C("q1"), ["pe", "q1"], ["fhi"], ["pe"])
        for k in (2, 3, 4, 5, 6, 7):
            count(k)
        sign(T.flo[:, 0:nc], T.pm3[:, 0:nc], -1.0, C("q0"), ["pm3", "q0"], ["flo"], ["pm3"])
        count(8)
        count(0)
        if t == 0:
            lin(C("u0", 2), C("d0", 2), 0.0625 if odd else -0.0625, 0.0, ["d0", "d1"], ["su"])
            if not odd:
                lin(C("s0", 2), C("d0", 2), -0.0625, COV / 16, ["d0", "d1"], ["sd"])
        lin(T.kt[:], T.kq[:], 1.0, apk, ["kq", "ap"], ["kt"])
        cc = (-8.0 + (8193.0 / 16 if t else -8191.0 / 16)) if odd else 9.0 - 8191.0 / 16
        dd = (-1.0 if t else 128.0) if odd else (0.0 if t else -129.0)
        lin(C("cc"), apk, 1.0, cc - ab, ["ap"], ["cc"])
        lin(C("dd"), apk, -1.0, dd + ab, ["ap"], ["dd"])
        lin(T.et[:], T.kt[:], 1.0, C("u%d" % t), ["kt", "su"], ["et"])
        if t == 0:
            lin(C("th1b"), C("th1p"), 1.0, C("th1"), ["th1p", "th1"], ["th1b"])
            if odd:
                lin(C("h1"), apk, 16.0, -16 * ab - 128.5, ["ap"], ["h1"])
                sign(T.vld[:, 0:120], T.nt[:, 0:120], -1.0, C("h1"), ["nt", "h1"], ["vla"])
            else:
                lin(C("h1"), apk, -16.0, 16 * ab - CAP - COV + 0.5, ["ap"], ["h1"])
                sign(T.vld[:, 9:NS], T.nt[:, 8:128], 1.0, C("h1"), ["nt", "h1"], ["vla"])
        s_after()

        ts(T.ai[:, 0:nc], val, -0.0625 - 0.47, -300.0, A.add, A.min, ["val"], ["ai"], ["px"])
        tt(T.xf[:, 0:nc], val, T.ai[:, 0:nc], A.subtract, ["val", "ai"], ["xf"], ["px"])
        for k in range(15):
            tk = T.tt[:, k * NT:k * NT + nc]
            ts(tk, T.xf[:, 0:nc], (k + 1) / 16.0, None, A.is_le, None, ["xf"], ["t%d" % k])
            mm(rr, T.rq[:, 15 - k:143 - k], tk, False, k == 14, ["rq0", "rq1", "t%d" % k], ["rr"], ["pz"])
            if k == FHI:
                mm(rr, T.idh[:], T.fhi[:, 0:nc], False, False, ["idh", "fhi"], ["rr"], ["pz"])
        ck2 = c[:, nc - 1:nc + 1] if odd else c[:, 0:2]
        mm(T.px[:, 404:408], T.one16[:], T.kc[:], True, False, ["one16", "kc0", "kc"], ["kk"], ["px"])
        mm(T.px[:, 404:406], T.one16[:], ck2, False, False, ck, ["kk"], ["px"])
        mm(T.px[:, 406:408], T.neg16[:], ck2, False, True, ["neg16"] + ck, ["kk"], ["px"])
        sk = ["ska%d" % t, "skb%d" % t]
        v_fill()
        a = (NT + 1) * t
        tt(T.lo[:, a:a + nc], rr, T.flo[:, 0:nc], A.add, ["rr", "flo"], ["lo"], ["pz"])
        tt(T.acs[:, 0:9], T.acc[:, 0:9], T.skip[:, 10 * t:10 * t + 9], A.add, ["acc%d" % k for k in range(9)] + sk,
           ["acs"])
        scan(T.mx[:, 0:nc + 1], T.lo[:, a:a + nc + 1], T.pz[:, 0:nc + 1], A.max, ["lo", "rr", "loz"], ["mx"], ["pz"])
        ts(T.el[:, 0:9], T.acs[:, 0:9], 0.5, None, A.mult, None, ["acs"], ["el"])
        ts(T.lw[:], T.mx[:, 0:nc + 1].indirect(T.el[:, 0:9]), U, None, A.mult, None, ["mx", "el"], ["lw"])


    def weave(*chains):
        for k in range(max(len(c) for c in chains)):
            for c in chains:
                if k < len(c):
                    c[k]()

    def place_list(t, a, b, outs):
        val, dw, du, dl = T.px[:, NT + a:NT + b], T.px[:, a:b], T.du[:, a:b], T["dl%d" % t]
        chain = [
            lambda: ts(du, val, C("cc"), C("dd"), A.is_ge if odd else A.is_lt, A.mult, ["val", "cc", "dd"], ["du"],
                       ["px"]),
            lambda: tt(dw, val, du, A.add, ["val", "du"], ["dw"], ["px"]),
            lambda: tt(du, dw, T["nq%d" % t][:, a:b], A.max if odd and t else A.min, ["dw", "nq%d" % t, "nq2"], ["du"],
                       ["px"])]
        for c, d, o in outs:
            chain.append(lambda c=c, d=d, o=o: ts(dl[:, c:d], T.du[:, c:d], 16.0, dconst[t] - o, A.mult, A.add, ["du"],
                                                  ["dl%d_%d" % (t, c)]))
        return chain

    def plain_list(t):
        ts(T.lpl[:, 0:9], T.kt[:], C(("u%d" if odd else "s%d") % t), 16.0, A.subtract, A.mult,
           ["kt", "su" if odd else "sd"], ["lpl"])

    kk, nk = (T.px[:, 405:406], T.px[:, 407:408]) if odd else (T.px[:, 404:405], T.px[:, 406:407])

    def far_list(t):
        ri = T.px[:, 401:402]
        return [
            lambda: ts(T.apn[:, 0:1], ri, abf - 0.47, None, A.add, None, ["kf"], ["apn"], ["px"]),
            lambda: ts(C("dl"), T.apn[:, 0:1], ri, nk, A.subtract, A.subtract, ["kf", "kk", "apn"], ["dl"], ["px"]),
            lambda: ts(T.eu[:], T.et[:], kk, C("dl"), A.is_ge if odd else A.is_lt, A.mult, ["et", "kk", "dl"], ["eu"],
                       ["px"]),
            lambda: tt(T.eu[:], T.et[:], T.eu[:], A.subtract, ["et", "eu"], ["eu"]),
            lambda: ts(T.ldy[:, 0:9], T.eu[:], 16.0, None, A.mult, None, ["eu"], ["ldy"])]

    def slot_flags():
        if odd:
            return [lambda: ts(T.vld[:, 120:NS], T.kt[:], kk, None, A.is_lt, None, ["kt", "kk"], ["vlb", "vlc"], ["px"])]
        return [
            lambda: ts(T.vld[:, 0:8], T.kt[:, 0:8], kk, None, A.is_ge, None, ["kt", "kk"], ["vlb"], ["px"]),
            lambda: ts(T.vld[:, 8:9], T.kt[:, 8:9], base / 16, None, A.is_lt, None, ["kt"], ["vlc"])]

    def piece(t, i):
        a, b = (CUM[t][i] + H) // 16, (CUM[t][i + 1] + H) // 16
        return (a, b) if odd else (128 - b, 128 - a)

    def depth(t, src, sk, add, z, zmid, zcov, plan, extra):
        w = T["w%d" % t]
        wa, wb, wc = T.wm[:, 3 * t, :], T.wm[:, 3 * t + 1, :], T.wm[:, 3 * t + 2, :]
        K = lambda s: "%s%d" % (s, t)
        ea = 0 if odd else 120
        cov = w[:, CV:CV + COV]
        nch = len(CUM[t]) - 1
        offsets_mm([(BANKS[i], chw(t, i)) for i in range(0 if t else 3, nch)] + [("pe", COV)])
        gather("V", cov, src, T.lw[:, 0:9], add, sk + ["lw"], [K("cov")])
        if far is not None:
            rl = relay_of(core, cores[far], cores, topo)
            if rl is None:
                send(cores[far], far_landing(T, t, far), cov, K("aC"), [K("cov")])
            else:
                send(rl, T["rl%d" % t][:], cov, K("rC"), [K("cov")])
        edge = w[:, MN + 16 * ea:MN + 16 * ea + H]
        gather("V", edge, src, T.lw[:, 10 + ea:18 + ea], add, sk + ["lw"], [K("edg")])
        nl = layout(near)
        na = nl[3] if odd else nl[0]
        send(cores[near], w[:, na:na + H], edge, K("aE"), [K("edg")])
        plain_list(t)
        own = [K("c%d_" % j) for j in range(nch)] + [K("edg"), K("cov"), K("near")]
        wn, wf = (wb, wc) if odd else (wc, wb)

        def task(e, name):
            kind = name[0]
            if kind in "cmpAMe":
                i = int(name[1])
                o, cw, b = cho(t, i), chw(t, i), BANKS[i]
                a = MN + o + (0 if odd else H)
                need = [K("c%d_" % i), K("c%d_" % (i - 1)) if i else K("edg")]
            if kind == "c":
                a, b = piece(t, i)
                gather(e, w[:, MN + 16 * a:MN + 16 * b], src, T.lw[:, 10 + a:10 + b], add, sk + ["lw"],
                       [K("c%d_" % i)])
            elif kind in "mp":
                k = 0 if (kind == "m") == odd else 1
                win = w[:, a:a + cw + H] if k else w[:, a - H:a + cw]
                k += 2 * t
                gather(e, T["x" + kind][:, o:o + cw], win, T.lmid[:, 32 * k:32 * k + cw // 16], 0,
                       need + ["lmid%d" % k] + ([K("near")] if name == "m0" else []), ["x" + name])
            elif kind == "A":
                mm(T[b][:, 0:cw], wa, w[:, a:a + cw], False, False, WM + need, [b], [b])
                mm(T[b][:, 0:cw], wf, T.xp[:, o:o + cw], False, False, ["xp%d" % i], [b], [b])
            elif kind == "M":
                mm(T[b][:, 0:cw], wn, T.xm[:, o:o + cw], False, True, ["xm%d" % i], [b], [b])
            elif kind == "e":
                clip(z[:, zmid + o:zmid + o + cw], T[b][:, 0:cw], [K("zm%d_" % i)], b)
            elif name == "Es":
                if odd:
                    gather(e, T.xme[:], w[:, 0:RH], T.lpl[:, 0:9], 0, own + ["lpl"], ["xme"])
                else:
                    gather(e, T.xme[:], w[:, COV:NW], T.lpl[:, 0:9], 0, own + [K("pad"), "lpl"], ["xme"])
            elif name == "Ev":
                gather(e, T.xpe[:], w[:], T.ldy[:, 0:9], 0, own + [K("pad"), K("far"), "ldy"], ["xpe"])
            elif name == "EM":
                mm(T.pe[:, 0:COV], wa, cov, False, False, WM + [K("cov")], ["pe"], ["pe"])
                mm(T.pe[:, 0:COV], wn, T.xme[:], False, False, ["xme"], ["pe"], ["pe"])
                mm(T.pe[:, 0:COV], wf, T.xpe[:], False, True, ["xpe"], ["pe"], ["pe"])
            elif name == "x8":
                s16 = "neg16" if odd else "one16"
                mm(T.px[:, 400:402], T[s16][:], T[K("ri")][:, 0:2], True, True, [s16, K("ri")], ["kf"], ["px"])
            elif name == "Ee":
                clip(z[:, zcov:zcov + COV], T.pe[:, 0:COV], [K("ze")], "pe")
            else:
                extra[name](e)

        cs = ["c%d" % i for i in range(nch)]
        pre = {"Es": cs, "Ev": cs + ["x2"], "EM": ["Es", "Ev"], "Ee": ["EM"]}
        for i in range(nch):
            pre["m%d" % i] = pre["p%d" % i] = cs[max(0, i - 1):i + 1]
            pre["A%d" % i] = ["p%d" % i]
            pre["M%d" % i] = ["m%d" % i, "A%d" % i]
            pre["e%d" % i] = ["M%d" % i]
        pre.update(extra["pre"])
        pre["x2"] = pre.get("x2", []) + ["x8"]
        pend = {"V": list(plan[0]), "S": list(plan[1]), "P": list(plan[2])}
        done = set()
        while pend["V"] or pend["S"] or pend["P"]:
            moved = False
            for e in "VSP":
                while pend[e] and all(x in done for x in pre.get(pend[e][0], [])):
                    task(e, pend[e][0])
                    done.add(pend[e].pop(0))
                    moved = True
            assert moved

    offsets_mm([(BANKS[i], chw(0, i)) for i in range(3)])
    scores(0, 0, T.xs, 0, XA, ["xa"])
    ts(T.xz[:, NZ + XS:NZ + XA], T.xs[:, XS:XA], OFF, None, A.add, None, ["xa"], ["x192a"])
    lin(T.xz[:, NZ:NZ + XS], T.xs[:, 0:XS], 1.0, OFF, ["xa"], ["x192c"])
    scores(0, XA // 16, T.xs, XA, S, ["xb"])
    ts(T.xz[:, NZ + XA:NZ + S], T.xs[:, XA:S], OFF, None, A.add, None, ["xb"], ["x192b"])
    cp(C("th0", 2), T.ths[:], ["ths"], ["th0", "th1"])
    keep("mk0", NT, "th0")
    lists(0, lambda: shift_lists(0), lambda: None)
    es = ["e%d" % i for i in range(len(CUM[0]) - 1)]
    zm = ["zm%d_0" % i for i in range(len(es))]
    cut = [CUM[0][2] // 16, NS]
    sa, sb = [(a, b) if odd else (NS - b, NS - a) for a, b in zip([0] + cut, cut)]
    z0 = zm + ["ze0"]

    def slot_scores(ab, rk):
        a, b = ab
        scores(1, a, T.xz, 16 * a, 16 * b, rk, (T.vld[:, a:b], ["vla", "vlb", "vlc"]))

    def expand(j):
        def run(e):
            a, b = span_of(YCUT, j)
            o = ycol(a)
            gather(e, T.yz[:, o:o + b - a], T.xz[:], T.dl0[:, a // 16:b // 16], 0,
                   z0 + ["x192a", "x192b", "x192c", "dl0_0"], ["y1_%d" % j])
        return run

    ex0 = {
        "x1": lambda e: weave(place_list(0, 0, NT, [(0, NT, 0)]), slot_flags()),
        "x2": lambda e: weave(far_list(0)),
        "x3": lambda e: slot_scores(sa, zm[0:2]),
        "x4": lambda e: slot_scores(sb, z0[2:]),
        "x5": lambda e: keep("mk1", NS, "th1b"),
        "y0": expand(0),
        "y1": expand(1),
        "pre": {"x3": es[0:2] + ["x1"], "x4": es[2:] + ["Ee", "x1"], "x5": ["x3", "x4", "x1"],
                "y0": es + ["Ee", "x1"], "y1": es + ["Ee", "x1"]},
    }
    depth(0, T.xs[:], ["xa", "xb"], 0, T.xz, 0 if odd else COV, MID if odd else 0, PLAN0, ex0)

    lists(1, lambda: expand(2)("V"), lambda: expand(3)("S"))
    ny = YCUT.index(TA)
    ys = [["y1_%d" % j for j in range(ny)], ["y1_%d" % j for j in range(len(YCUT) - 1)]]
    part_of = [0 if FCUT[j] < TA else 1 for j in range(len(FNEED))]

    def fwin(j):
        c, late = FNEED[j], part_of[j]
        if odd:
            return 0 if late else S - TA, S + COV + CUM[1][c + 1]
        return cho(1, c), NZ + (S if late else TA)

    def outs(k):
        by = {}
        for j in range(len(FNEED)):
            if part_of[j] == k:
                by.setdefault(fwin(j)[0], []).extend(span_of(FCUT, j))
        return [(min(v) // 16, max(v) // 16, o) for o, v in by.items()]

    def final(j):
        def run(e):
            a, b = span_of(FCUT, j)
            c, d = fwin(j)
            dl = ["dl1_%d" % x[0] for x in outs(part_of[j]) if x[2] == c]
            gather(e, T.ysb[:, a:b], T.yz[:, c:d], T.dl1[:, a // 16:b // 16], -OFF,
                   ["zm%d_1" % i for i in range(FNEED[j] + 1)] + ["ze1"] + dl + ys[part_of[j]], ["ysb%d" % j])
        return run

    def token_scores(k):
        a, b = PART[k]
        scores(1, a // 16, T.yz, ycol(a), ycol(a) + b - a, ys[k], (T.mk0[:, a // 16:b // 16], ["mk0"]))

    def token_places(k):
        a, b = PART[k][0] // 16, PART[k][1] // 16
        mk, val, cx = T.mk2[:, a:b], T.px[:, NT + a:NT + b], T.cz[:, 1 + a:1 + b]
        up = "up16b" if odd else "up16"
        ts(mk, T.py[:, SC + a:SC + b], C("th1b"), None, A.is_ge, None, ["sco", "th1b"], ["mk2"], ["py"])
        mm(val, T[up][:], mk, True, False, [up, "mk2"], ["val"], ["px"])
        init = T.cz[:, a:a + 1] if odd and k else 0.0
        op("V", lambda: g.vector.tensor_tensor_scan(cx, mk, mk, init, A.add, A.max), ["mk2"] + ["cz"] * k, ["cz"])
        if not odd:
            cy = T.cy[:, 1 + a:1 + b]
            if k:
                ts(cy, cx, T.cz[:, b:b + 1], T.cz[:, NT:NT + 1], A.subtract, A.subtract, ["cz"], ["cy"])
            else:
                ts(cy, cx, T.cz[:, b:b + 1], None, A.subtract, None, ["cz"], ["cy"])
            cx = cy
        mm(val, T.one16[:], cx, False, True, ["one16", "cz" if odd else "cy"], ["val"], ["px"])

    def before(x):
        return PLAN1[2][:PLAN1[2].index(x)]

    ca, cb = [(a // 16, b // 16) for a, b in PART]
    ex1 = {
        "y4": expand(4),
        "y5": expand(5),
        "x1": lambda e: token_scores(0),
        "x3": lambda e: token_places(0),
        "x2": lambda e: weave(place_list(1, ca[0], ca[1], outs(0)), far_list(1)),
        "z1": lambda e: token_scores(1),
        "z3": lambda e: token_places(1),
        "z2": lambda e: weave(place_list(1, cb[0], cb[1], outs(1))),
        "x7": lambda e: None,
        "z7": lambda e: None,
        "pre": {"x3": before("x7") + ["x1"], "x7": ["x3"], "x2": ["x3"], "z1": ["y4", "y5", "x3"],
                "x1": ["y%d" % j for j in range(4, ny)],
                "z3": (before("z7") if TA < S else []) + ["z1", "x2"], "z7": ["z3"], "z2": ["z3"]},
    }
    for j in range(len(FNEED)):
        ex1["f%d" % j] = final(j)
        ex1["pre"]["f%d" % j] = ["e%d" % i for i in range(FNEED[j] + 1)] + ["Ee", "z2" if part_of[j] else "x2"]
    depth(1, T.xz[:, 0:NZ], z0, -OFF, T.yz, S + COV if odd else 0, S if odd else MID, PLAN1, ex1)
    for js in STORES:
        a, b = min(span_of(FCUT, j)[0] for j in js), max(span_of(FCUT, j)[1] for j in js)
        wait("Y", deps("Y", ["ysb%d" % j for j in js], (), ()))
        g.sync.dma_start(T.y[:, a:b], T.ysb[:, a:b]).then_inc(T.sem.dst, 16)
    wait("G", [("c" + e, cnt[e]) for e in cnt] + [("sent", sent[0]), ("dst", 16 * len(STORES))])
